import numpy as np
import ml_dtypes


def mxq(x, axis, fmt="e4m3"):
    dtype, down = {"e4m3": (ml_dtypes.float8_e4m3fn, 7), "e5m2": (ml_dtypes.float8_e5m2, 14)}[fmt]
    v = np.moveaxis(np.asarray(x, np.float32).astype(ml_dtypes.bfloat16).astype(np.float64), axis, -1)
    blocks = v.reshape(v.shape[:-1] + (-1, 32))
    amax = np.abs(blocks).max(-1, keepdims=True)
    byte = np.maximum(np.where(amax > 0, np.frexp(amax)[1] - 1 + 127, 0) - down, 1)
    scale = np.exp2(byte - 127.0)
    codes = (blocks / scale).astype(np.float32).astype(dtype).astype(np.float64)
    return np.moveaxis((codes * scale).reshape(v.shape), -1, axis)


WIDE = False


def mx_kscale(k):
    if not WIDE:
        return np.ones(k)
    levels = np.array([24, -24, 12, -12, 0])
    if k % 512:
        return np.exp2(np.random.permutation(np.resize(levels, k // 32))).repeat(32)
    a = np.empty((k // 512, 16))
    for p in range(k // 512):
        a[p, :8] = np.random.permutation(np.resize(levels, 8))
        for g in range(8):
            far = levels[np.abs(levels - a[p, g]) >= 10]
            a[p, g + 8] = far[np.random.randint(len(far))]
    return np.exp2(a.ravel()).repeat(32)


def f64(x):
    return np.asarray(x).astype(np.float64)


K, N, T = 1024, 1024, 1536


def setup_inputs():
    n = np.random.standard_normal
    s = mx_kscale(K)[:, None]
    return {
        "w": (n((K, N)) / np.sqrt(K) / s).astype(np.float32),
        "x": (n((K, T)) * s).astype(np.float32),
    }


def reference(w, x):
    w_q_ = mxq(f64(w), 0, "e4m3")
    w_r_ = mxq(f64(w) - w_q_, 0, "e4m3")
    x_ = mxq(f64(x), 0, "e4m3")
    y = w_q_.T @ x_ + w_r_.T @ x_
    return (np.maximum(y, 0.0)) ** 2

@@ -1,0 +1,236 @@
+from contextlib import ExitStack
+
+import concourse.mybir as mybir
+
+K, N, T = 1024, 1024, 1536
+FLOPS = 2 * 2 * K * N * T
+
+F32 = mybir.dt.float32
+BF16 = mybir.dt.bfloat16
+U32 = mybir.dt.uint32
+U8 = mybir.dt.uint8
+FP8X4 = mybir.dt.float8_e4m3fn_x4
+ALU = mybir.AluOpType
+ACT = mybir.ActivationFunctionType
+
+P = 128
+PACK = 4
+K_PASS = P * PACK
+PASSES = K // K_PASS
+CHUNK = 256
+T_TILE = 512
+PAIR = 2
+
+
+def tile_mix_tierw_relu2_kernel(tc, w, x, out):
+    nc = tc.nc
+    with ExitStack() as ctx:
+        keep = ctx.enter_context(tc.tile_pool(name="keep", bufs=1))
+        stage = ctx.enter_context(tc.tile_pool(name="stage", bufs=6))
+        psum = ctx.enter_context(tc.psum_pool(name="psum", bufs=1))
+        free_banks = list(range(8))
+        bank_of = {}
+        ctx.enter_context(tc.manual_schedule())
+
+        raw, grouped, codes, scales = {}, {}, {}, {}
+        deq, resid, acc, res = {}, {}, {}, {}
+
+        def by_pairs_rows(ap):
+            return ap.rearrange("p t (c i) -> p c t i", i=PAIR)
+
+        def by_pairs_words(ap):
+            return ap.rearrange("p (c i t) -> p c t i", i=PAIR, t=PACK)
+
+        def L(u):
+            name, c, g = u
+            src = w if name == "w" else x
+            raw[u] = keep.tile([P, PACK, CHUNK], F32, name="raw_%s_%d_%d" % u)
+            rows = src[g * K_PASS : (g + 1) * K_PASS, c * CHUNK : (c + 1) * CHUNK]
+            nc.sync.dma_start(out=raw[u][:], in_=rows.rearrange("(p j) n -> p j n", j=PACK))
+
+        def C(u, eng, lo=0, hi=CHUNK):
+            if u not in grouped:
+                grouped[u] = stage.tile([P, PACK * CHUNK], BF16, name="grouped", align_bytes=64)
+            dst = by_pairs_words(grouped[u][:, PACK * lo : PACK * hi])
+            src = by_pairs_rows(raw[u][:, :, lo:hi])
+            if eng == "V":
+                nc.vector.tensor_copy(out=dst, in_=src)
+            elif eng == "G":
+                nc.gpsimd.tensor_scalar(out=dst, in0=src, scalar1=1.0, scalar2=0.0, op0=ALU.mult, op1=ALU.add)
+            else:
+                nc.scalar.copy(out=dst, in_=src)
+
+        def planes(key, width):
+            if key not in codes:
+                codes[key] = keep.tile([P, width], U32, name="codes_%s_%d_%d" % key, align_bytes=256)
+                scales[key] = keep.tile([P, width], U8, name="scales_%s_%d_%d" % key, align_bytes=256)
+            return codes[key], scales[key]
+
+        def Q(u):
+            name, c, g = u
+            if name == "w":
+                cd, sc = planes(u, CHUNK)
+                cols = slice(0, CHUNK)
+            else:
+                cd, sc = planes(("x", c // 2, g), T_TILE)
+                cols = slice((c % 2) * CHUNK, (c % 2 + 1) * CHUNK)
+            nc.vector.quantize_mx(out=cd[:, cols].bitcast(FP8X4), scales=sc[:, cols], in_=grouped[u][:])
+
+        def DQ(i, g):
+            cols = slice((i % 2) * P, (i % 2 + 1) * P)
+            bank_of["d", i, g] = free_banks.pop(0)
+            deq[i, g] = psum.tile([P, PACK, P], F32, name="bank_%d" % bank_of["d", i, g])
+            for j in range(PACK):
+                nc.tensor.matmul_mx(
+                    out=deq[i, g][:, j, :],
+                    lhsT=id_codes[:, j * P : (j + 1) * P].bitcast(FP8X4),
+                    lhsT_scale=id_scales[:, j * P : (j + 1) * P],
+                    rhs=codes["w", i // 2, g][:, cols].bitcast(FP8X4),
+                    rhs_scale=scales["w", i // 2, g][:, cols],
+                    start=True,
+                    stop=True,
+                )
+
+        def SUB(i, g):
+            c, h = divmod(i, 2)
+            if (c, g) not in resid:
+                resid[c, g] = stage.tile([P, PACK * CHUNK], BF16, name="resid", bufs=3, align_bytes=64)
+            nc.vector.tensor_tensor(
+                out=by_pairs_words(resid[c, g][:, h * K_PASS : (h + 1) * K_PASS]),
+                in0=by_pairs_rows(raw["w", c, g][:, :, h * P : (h + 1) * P]),
+                in1=by_pairs_rows(deq[i, g][:]),
+                op=ALU.subtract,
+            )
+            free_banks.append(bank_of["d", i, g])
+
+        def QR(c, g):
+            cd, sc = planes(("r", c, g), CHUNK)
+            nc.vector.quantize_mx(out=cd[:].bitcast(FP8X4), scales=sc[:], in_=resid[c, g][:])
+
+        def MM(i, t, g, tier):
+            first = (i, t) not in acc
+            if first:
+                bank_of["a", i, t] = free_banks.pop(0)
+                bank = psum.tile([P, T_TILE], F32, name="bank_%d" % bank_of["a", i, t])
+                acc[i, t] = [bank, 0]
+            acc[i, t][1] = acc[i, t][1] + 1
+            key = ("wr"[tier], i // 2, g)
+            cols = slice((i % 2) * P, (i % 2 + 1) * P)
+            nc.tensor.matmul_mx(
+                out=acc[i, t][0][:],
+                lhsT=codes[key][:, cols].bitcast(FP8X4),
+                lhsT_scale=scales[key][:, cols],
+                rhs=codes["x", t, g][:].bitcast(FP8X4),
+                rhs_scale=scales["x", t, g][:],
+                start=first,
+                stop=acc[i, t][1] == 2 * PASSES,
+            )
+
+        def R(i, t, eng, lo=0, hi=T_TILE):
+            if i not in res:
+                res[i] = keep.tile([P, T], F32, name="res_%d" % i)
+            dst = res[i][:, t * T_TILE + lo : t * T_TILE + hi]
+            if eng == "V":
+                nc.vector.tensor_scalar_max(out=dst, in0=acc[i, t][0][:, lo:hi], scalar1=0.0)
+            else:
+                nc.scalar.activation(out=dst, in_=acc[i, t][0][:, lo:hi], func=ACT.Relu)
+            if hi == T_TILE:
+                free_banks.append(bank_of["a", i, t])
+
+        def SQ(i, t, eng, lo=0, hi=T_TILE):
+            dst = res[i][:, t * T_TILE + lo : t * T_TILE + hi]
+            if eng == "V":
+                nc.vector.tensor_tensor(out=dst, in0=dst, in1=dst, op=ALU.mult)
+            elif eng == "G":
+                nc.gpsimd.tensor_tensor(out=dst, in0=dst, in1=dst, op=ALU.mult)
+            else:
+                nc.scalar.activation(out=dst, in_=dst, func=ACT.Square)
+
+        def ST(i, lo, hi):
+            nc.sync.dma_start(out=out[i * P : (i + 1) * P, lo:hi], in_=res[i][:, lo:hi])
+
+        def IDENT():
+            ramp = keep.tile([P, K_PASS + PACK], BF16, name="ramp")
+            nc.gpsimd.memset(ramp[:], 0.0)
+            nc.gpsimd.affine_select(
+                out=ramp[:], in_=ramp[:], compare_op=ALU.not_equal, fill=1.0,
+                base=PACK - 1, pattern=[[-1, K_PASS + PACK]], channel_multiplier=PACK,
+            )
+            ident = keep.tile([P, PACK * K_PASS], BF16, name="ident", align_bytes=64)
+            for j in range(PACK):
+                dst = ident[:, j * K_PASS : (j + 1) * K_PASS]
+                src = ramp[:, PACK - 1 - j : PACK - 1 - j + K_PASS]
+                if j == 0:
+                    nc.scalar.activation(out=dst, in_=src, func=ACT.Square)
+                else:
+                    nc.vector.tensor_copy(out=dst, in_=src)
+            nc.vector.quantize_mx(out=id_codes[:].bitcast(FP8X4), scales=id_scales[:], in_=ident[:])
+
+        id_codes = keep.tile([P, K_PASS], U32, name="id_codes", align_bytes=256)
+        id_scales = keep.tile([P, K_PASS], U8, name="id_scales", align_bytes=256)
+
+
+        WA = [("w", 0, 0), ("w", 1, 0), ("w", 0, 1), ("w", 1, 1)]
+        WB = [("w", 2, 0), ("w", 2, 1), ("w", 3, 0), ("w", 3, 1)]
+        X = [("x", 2 * t + h, g) for t in range(3) for g in (0, 1) for h in (0, 1)]
+        for u in WA + X[:8] + WB + X[8:]:
+            L(u)
+        IDENT()
+
+        def D2(u):
+            DQ(2 * u[1], u[2])
+            DQ(2 * u[1] + 1, u[2])
+
+        def S1(u, h):
+            SUB(2 * u[1] + h, u[2])
+
+        def Q2(u):
+            QR(u[1], u[2])
+
+        def M(tiles, ts, g, p):
+            for i in tiles:
+                for t in ts:
+                    MM(i, t, g, p)
+
+        A = range(4)
+        C(WA[0], "V", 0, 160); C(WA[0], "S", 160, 256); Q(WA[0]); D2(WA[0])
+        for u in WA[1:] + X[:2]:
+            C(u, "S")
+        S1(WA[0], 0); Q(WA[1]); D2(WA[1]); S1(WA[0], 1); Q(WA[2]); D2(WA[2]); Q2(WA[0])
+        S1(WA[1], 0); Q(WA[3]); S1(WA[1], 1); D2(WA[3]); Q(X[0]); Q2(WA[1])
+        for u in X[2:5]:
+            C(u, "S")
+        S1(WA[2], 0); Q(X[1]); M(A, (0,), 0, 0); M(A, (0,), 0, 1); S1(WA[2], 1); S1(WA[3], 0); Q(X[2]); Q2(WA[2]); Q(X[3]); S1(WA[3], 1)
+        M(A, (0,), 1, 0)
+        C(X[5], "V"); Q2(WA[3]); M(A, (0,), 1, 1); Q(X[4]); Q(X[5])
+        C(X[6], "S")
+        for i in A:
+            M((i,), (1,), 0, 0); M((i,), (1,), 0, 1)
+        R(0, 0, "V"); C(X[7], "V"); Q(X[6]); R(1, 0, "S"); R(2, 0, "S"); R(3, 0, "V"); Q(X[7])
+        C(WB[0], "S"); C(WB[1], "S"); SQ(0, 0, "V"); Q(WB[0])
+        for i in A:
+            M((i,), (1,), 1, 0); M((i,), (1,), 1, 1)
+            if i == 1:
+                D2(WB[0])
+        R(0, 1, "V"); Q(WB[1]); D2(WB[1]); S1(WB[0], 0); S1(WB[0], 1); R(1, 1, "S"); R(2, 1, "S"); R(3, 1, "S")
+        C(WB[2], "S"); C(WB[3], "S")
+        M((4, 5), (0, 1), 0, 0); S1(WB[1], 0); Q2(WB[0]); S1(WB[1], 1); Q(WB[2])
+        M((4, 5), (0, 1), 1, 0); M((4, 5), (0, 1), 0, 1); D2(WB[2]); Q2(WB[1]); Q(WB[3])
+        S1(WB[2], 0); S1(WB[2], 1); M((4,), (0, 1), 1, 1); D2(WB[3]); M((5,), (0, 1), 1, 1)
+        SQ(0, 1, "S"); ST(0, 0, 1024)
+        R(4, 0, "S"); R(4, 1, "S")
+        S1(WB[3], 0); Q2(WB[2]); S1(WB[3], 1); C(X[8], "V"); Q2(WB[3])
+        R(5, 0, "S"); R(5, 1, "S")
+        M((6,), (0, 1), 0, 0); M((6,), (0, 1), 1, 0); M((6,), (0, 1), 0, 1); M((6,), (0, 1), 1, 1)
+        for i in (1, 2, 3):
+            SQ(i, 0, "S", 0, 1024); ST(i, 0, 1024)
+        M((7,), (0, 1), 0, 0); M((7,), (0, 1), 1, 0); M((7,), (0, 1), 0, 1); M((7,), (0, 1), 1, 1)
+        C(X[9], "V"); Q(X[8]); Q(X[9]); C(X[10], "V"); C(X[11], "V"); Q(X[10]); R(6, 0, "V"); Q(X[11]); R(6, 1, "V")
+        SQ(4, 0, "S", 0, 1024); ST(4, 0, 1024)
+        R(7, 0, "V"); R(7, 1, "V")
+        for i in range(8):
+            for g in (0, 1):
+                M((i,), (2,), g, 0); M((i,), (2,), g, 1)
+            if i < 3:
+                SQ(5 + i, 0, "V"); SQ(5 + i, 1, "S"); ST(5 + i, 0, 1024)
+            R(i, 2, "V"); SQ(i, 2, "S"); ST(i, 1024, 1536)

@@ -26,7 +26,7 @@ def tile_mix_tierw_relu2_kernel(tc, w, x, out):
     nc = tc.nc
     with ExitStack() as ctx:
         keep = ctx.enter_context(tc.tile_pool(name="keep", bufs=1))
-        stage = ctx.enter_context(tc.tile_pool(name="stage", bufs=6))
+        stage = ctx.enter_context(tc.tile_pool(name="stage", bufs=8))
         psum = ctx.enter_context(tc.psum_pool(name="psum", bufs=1))
         free_banks = list(range(8))
         bank_of = {}
@@ -47,6 +47,15 @@ def tile_mix_tierw_relu2_kernel(tc, w, x, out):
             raw[u] = keep.tile([P, PACK, CHUNK], F32, name="raw_%s_%d_%d" % u)
             rows = src[g * K_PASS : (g + 1) * K_PASS, c * CHUNK : (c + 1) * CHUNK]
             nc.sync.dma_start(out=raw[u][:], in_=rows.rearrange("(p j) n -> p j n", j=PACK))
+
+        def L2(u, v):
+            name, c, g = u
+            src = w if name == "w" else x
+            both = keep.tile([P, PACK, 2 * CHUNK], F32, name="raw_%s_%d_%d" % u)
+            rows = src[g * K_PASS : (g + 1) * K_PASS, c * CHUNK : (c + 2) * CHUNK]
+            nc.sync.dma_start(out=both[:], in_=rows.rearrange("(p j) n -> p j n", j=PACK))
+            raw[u] = both[:, :, 0:CHUNK]
+            raw[v] = both[:, :, CHUNK : 2 * CHUNK]
 
         def C(u, eng, lo=0, hi=CHUNK):
             if u not in grouped:
@@ -107,11 +116,12 @@ def tile_mix_tierw_relu2_kernel(tc, w, x, out):
             cd, sc = planes(("r", c, g), CHUNK)
             nc.vector.quantize_mx(out=cd[:].bitcast(FP8X4), scales=sc[:], in_=resid[c, g][:])
 
-        def MM(i, t, g, tier):
+        def MM(i, tt, g, tier, lo=0, hi=T_TILE):
+            t = (tt, lo)
             first = (i, t) not in acc
             if first:
                 bank_of["a", i, t] = free_banks.pop(0)
-                bank = psum.tile([P, T_TILE], F32, name="bank_%d" % bank_of["a", i, t])
+                bank = psum.tile([P, hi - lo], F32, name="bank_%d" % bank_of["a", i, t])
                 acc[i, t] = [bank, 0]
             acc[i, t][1] = acc[i, t][1] + 1
             key = ("wr"[tier], i // 2, g)
@@ -120,8 +130,8 @@ def tile_mix_tierw_relu2_kernel(tc, w, x, out):
                 out=acc[i, t][0][:],
                 lhsT=codes[key][:, cols].bitcast(FP8X4),
                 lhsT_scale=scales[key][:, cols],
-                rhs=codes["x", t, g][:].bitcast(FP8X4),
-                rhs_scale=scales["x", t, g][:],
+                rhs=codes["x", tt, g][:, lo:hi].bitcast(FP8X4),
+                rhs_scale=scales["x", tt, g][:, lo:hi],
                 start=first,
                 stop=acc[i, t][1] == 2 * PASSES,
             )
@@ -131,11 +141,10 @@ def tile_mix_tierw_relu2_kernel(tc, w, x, out):
                 res[i] = keep.tile([P, T], F32, name="res_%d" % i)
             dst = res[i][:, t * T_TILE + lo : t * T_TILE + hi]
             if eng == "V":
-                nc.vector.tensor_scalar_max(out=dst, in0=acc[i, t][0][:, lo:hi], scalar1=0.0)
+                nc.vector.tensor_scalar_max(out=dst, in0=acc[i, (t, lo)][0][:], scalar1=0.0)
             else:
-                nc.scalar.activation(out=dst, in_=acc[i, t][0][:, lo:hi], func=ACT.Relu)
-            if hi == T_TILE:
-                free_banks.append(bank_of["a", i, t])
+                nc.scalar.activation(out=dst, in_=acc[i, (t, lo)][0][:], func=ACT.Relu)
+            free_banks.append(bank_of["a", i, (t, lo)])
 
         def SQ(i, t, eng, lo=0, hi=T_TILE):
             dst = res[i][:, t * T_TILE + lo : t * T_TILE + hi]
@@ -173,9 +182,6 @@ def tile_mix_tierw_relu2_kernel(tc, w, x, out):
         WA = [("w", 0, 0), ("w", 1, 0), ("w", 0, 1), ("w", 1, 1)]
         WB = [("w", 2, 0), ("w", 2, 1), ("w", 3, 0), ("w", 3, 1)]
         X = [("x", 2 * t + h, g) for t in range(3) for g in (0, 1) for h in (0, 1)]
-        for u in WA + X[:8] + WB + X[8:]:
-            L(u)
-        IDENT()
 
         def D2(u):
             DQ(2 * u[1], u[2])
@@ -193,44 +199,55 @@ def tile_mix_tierw_relu2_kernel(tc, w, x, out):
                     MM(i, t, g, p)
 
         A = range(4)
+
+        L(WA[0]); L(WA[1]); L2(WA[2], WA[3]); L2(X[0], X[1]); L2(X[2], X[3]); L2(X[4], X[5]); L2(X[6], X[7]); L2(WB[0], WB[2]); L2(WB[1], WB[3]); L2(X[8], X[9]); L2(X[10], X[11])
+        IDENT()
         C(WA[0], "V", 0, 160); C(WA[0], "S", 160, 256); Q(WA[0]); D2(WA[0])
-        for u in WA[1:] + X[:2]:
+        for u in [WA[1], WA[2], WA[3], X[0], X[2]]:
             C(u, "S")
-        S1(WA[0], 0); Q(WA[1]); D2(WA[1]); S1(WA[0], 1); Q(WA[2]); D2(WA[2]); Q2(WA[0])
-        S1(WA[1], 0); Q(WA[3]); S1(WA[1], 1); D2(WA[3]); Q(X[0]); Q2(WA[1])
-        for u in X[2:5]:
-            C(u, "S")
-        S1(WA[2], 0); Q(X[1]); M(A, (0,), 0, 0); M(A, (0,), 0, 1); S1(WA[2], 1); S1(WA[3], 0); Q(X[2]); Q2(WA[2]); Q(X[3]); S1(WA[3], 1)
-        M(A, (0,), 1, 0)
-        C(X[5], "V"); Q2(WA[3]); M(A, (0,), 1, 1); Q(X[4]); Q(X[5])
-        C(X[6], "S")
+        C(X[3], "S", 128, 256); C(X[4], "S"); C(X[5], "S")
+        S1(WA[0], 0); Q(WA[1]); D2(WA[1]); S1(WA[0], 1); Q2(WA[0]); S1(WA[1], 0); Q(WA[2]); D2(WA[2]); S1(WA[1], 1); C(X[1], "V"); Q(WA[3]); D2(WA[3]); Q(X[1]); Q(X[0]); Q2(WA[1])
+        M(A, (0,), 0, 0); M(A, (0,), 0, 1)
+        S1(WA[2], 0); C(X[3], "V", 0, 128); S1(WA[2], 1); Q(X[2]); Q2(WA[2]); Q(X[3]); S1(WA[3], 0); S1(WA[3], 1); Q(X[4]); Q2(WA[3]); Q(X[5]); C(X[7], "V")
+        M(A, (0,), 1, 0); M(A, (0,), 1, 1)
+        C(X[6], "V"); Q(X[7])
+        for i in A:
+            R(i, 0, "S")
         for i in A:
             M((i,), (1,), 0, 0); M((i,), (1,), 0, 1)
-        R(0, 0, "V"); C(X[7], "V"); Q(X[6]); R(1, 0, "S"); R(2, 0, "S"); R(3, 0, "V"); Q(X[7])
-        C(WB[0], "S"); C(WB[1], "S"); SQ(0, 0, "V"); Q(WB[0])
+        Q(X[6])
+        C(WB[0], "V"); C(WB[2], "S"); Q(WB[0]); Q(WB[2])
         for i in A:
             M((i,), (1,), 1, 0); M((i,), (1,), 1, 1)
             if i == 1:
                 D2(WB[0])
-        R(0, 1, "V"); Q(WB[1]); D2(WB[1]); S1(WB[0], 0); S1(WB[0], 1); R(1, 1, "S"); R(2, 1, "S"); R(3, 1, "S")
-        C(WB[2], "S"); C(WB[3], "S")
-        M((4, 5), (0, 1), 0, 0); S1(WB[1], 0); Q2(WB[0]); S1(WB[1], 1); Q(WB[2])
-        M((4, 5), (0, 1), 1, 0); M((4, 5), (0, 1), 0, 1); D2(WB[2]); Q2(WB[1]); Q(WB[3])
-        S1(WB[2], 0); S1(WB[2], 1); M((4,), (0, 1), 1, 1); D2(WB[3]); M((5,), (0, 1), 1, 1)
-        SQ(0, 1, "S"); ST(0, 0, 1024)
-        R(4, 0, "S"); R(4, 1, "S")
-        S1(WB[3], 0); Q2(WB[2]); S1(WB[3], 1); C(X[8], "V"); Q2(WB[3])
-        R(5, 0, "S"); R(5, 1, "S")
-        M((6,), (0, 1), 0, 0); M((6,), (0, 1), 1, 0); M((6,), (0, 1), 0, 1); M((6,), (0, 1), 1, 1)
-        for i in (1, 2, 3):
+            if i == 2:
+                D2(WB[2])
+        S1(WB[0], 0); C(WB[1], "V"); S1(WB[0], 1); Q(WB[1]); Q2(WB[0])
+        for i in A:
+            R(i, 1, "S")
+        C(WB[3], "S")
+        M((4,), (0, 1), 0, 0); D2(WB[1]); M((5,), (0, 1), 0, 0); S1(WB[2], 0); S1(WB[2], 1); S1(WB[1], 0); Q(WB[3]); S1(WB[1], 1); Q2(WB[2]); Q2(WB[1])
+        M((4, 5), (0, 1), 0, 1); D2(WB[3]); M((4, 5), (0, 1), 1, 0); M((4, 5), (0, 1), 1, 1)
+        for i in A:
             SQ(i, 0, "S", 0, 1024); ST(i, 0, 1024)
-        M((7,), (0, 1), 0, 0); M((7,), (0, 1), 1, 0); M((7,), (0, 1), 0, 1); M((7,), (0, 1), 1, 1)
-        C(X[9], "V"); Q(X[8]); Q(X[9]); C(X[10], "V"); C(X[11], "V"); Q(X[10]); R(6, 0, "V"); Q(X[11]); R(6, 1, "V")
-        SQ(4, 0, "S", 0, 1024); ST(4, 0, 1024)
-        R(7, 0, "V"); R(7, 1, "V")
-        for i in range(8):
+        S1(WB[3], 0); S1(WB[3], 1); C(X[8], "V"); Q2(WB[3]); C(X[9], "V"); Q(X[8]); Q(X[9])
+        C(X[10], "V"); C(X[11], "V"); Q(X[10]); Q(X[11])
+        for i in (4, 5):
+            R(i, 0, "S"); R(i, 1, "S")
+        for i in (6, 7):
+            M((i,), (0, 1), 0, 0); M((i,), (0, 1), 1, 0); M((i,), (0, 1), 0, 1); M((i,), (0, 1), 1, 1)
+        for i in (4, 5):
+            SQ(i, 0, "S", 0, 1024); ST(i, 0, 1024)
+        for i in (6, 7):
+            R(i, 0, "V"); R(i, 1, "V"); SQ(i, 0, "S", 0, 1024); ST(i, 0, 1024)
+
+        for i in range(6):
             for g in (0, 1):
                 M((i,), (2,), g, 0); M((i,), (2,), g, 1)
-            if i < 3:
-                SQ(5 + i, 0, "V"); SQ(5 + i, 1, "S"); ST(5 + i, 0, 1024)
             R(i, 2, "V"); SQ(i, 2, "S"); ST(i, 1024, 1536)
+        for i in (6, 7):
+            for lo in (0, 256):
+                for g in (0, 1):
+                    MM(i, 2, g, 0, lo, lo + 256); MM(i, 2, g, 1, lo, lo + 256)
+                R(i, 2, "V", lo, lo + 256); SQ(i, 2, "S", lo, lo + 256); ST(i, 1024 + lo, 1280 + lo)

@@ -19,7 +19,7 @@ K_PASS = P * PACK
 PASSES = K // K_PASS
 CHUNK = 256
 T_TILE = 512
-PAIR = 2
+PAIR = 4
 
 
 def tile_mix_tierw_relu2_kernel(tc, w, x, out):
@@ -227,8 +227,8 @@ def tile_mix_tierw_relu2_kernel(tc, w, x, out):
         for i in A:
             R(i, 1, "S")
         C(WB[3], "S")
-        M((4,), (0, 1), 0, 0); D2(WB[1]); M((5,), (0, 1), 0, 0); S1(WB[2], 0); S1(WB[2], 1); S1(WB[1], 0); Q(WB[3]); S1(WB[1], 1); Q2(WB[2]); Q2(WB[1])
-        M((4, 5), (0, 1), 0, 1); D2(WB[3]); M((4, 5), (0, 1), 1, 0); M((4, 5), (0, 1), 1, 1)
+        M((4, 5), (0, 1), 0, 0); D2(WB[1]); S1(WB[2], 0); S1(WB[2], 1); S1(WB[1], 0); Q(WB[3]); S1(WB[1], 1); Q2(WB[2]); Q2(WB[1])
+        M((4, 5), (0, 1), 0, 1); M((4,), (0, 1), 1, 0); D2(WB[3]); M((5,), (0, 1), 1, 0); M((4, 5), (0, 1), 1, 1)
         for i in A:
             SQ(i, 0, "S", 0, 1024); ST(i, 0, 1024)
         S1(WB[3], 0); S1(WB[3], 1); C(X[8], "V"); Q2(WB[3]); C(X[9], "V"); Q(X[8]); Q(X[9])

@@ -41,21 +41,13 @@ def tile_mix_tierw_relu2_kernel(tc, w, x, out):
         def by_pairs_words(ap):
             return ap.rearrange("p (c i t) -> p c t i", i=PAIR, t=PACK)
 
-        def L(u):
-            name, c, g = u
+        def LD(name, c0, c1, g):
             src = w if name == "w" else x
-            raw[u] = keep.tile([P, PACK, CHUNK], F32, name="raw_%s_%d_%d" % u)
-            rows = src[g * K_PASS : (g + 1) * K_PASS, c * CHUNK : (c + 1) * CHUNK]
-            nc.sync.dma_start(out=raw[u][:], in_=rows.rearrange("(p j) n -> p j n", j=PACK))
-
-        def L2(u, v):
-            name, c, g = u
-            src = w if name == "w" else x
-            both = keep.tile([P, PACK, 2 * CHUNK], F32, name="raw_%s_%d_%d" % u)
-            rows = src[g * K_PASS : (g + 1) * K_PASS, c * CHUNK : (c + 2) * CHUNK]
-            nc.sync.dma_start(out=both[:], in_=rows.rearrange("(p j) n -> p j n", j=PACK))
-            raw[u] = both[:, :, 0:CHUNK]
-            raw[v] = both[:, :, CHUNK : 2 * CHUNK]
+            panel = keep.tile([P, PACK, (c1 - c0) * CHUNK], F32, name="raw_%s_%d_%d" % (name, c0, g))
+            rows = src[g * K_PASS : (g + 1) * K_PASS, c0 * CHUNK : c1 * CHUNK]
+            nc.sync.dma_start(out=panel[:], in_=rows.rearrange("(p j) n -> p j n", j=PACK))
+            for c in range(c0, c1):
+                raw[name, c, g] = panel[:, :, (c - c0) * CHUNK : (c - c0 + 1) * CHUNK]
 
         def C(u, eng, lo=0, hi=CHUNK):
             if u not in grouped:
@@ -75,15 +67,17 @@ def tile_mix_tierw_relu2_kernel(tc, w, x, out):
                 scales[key] = keep.tile([P, width], U8, name="scales_%s_%d_%d" % key, align_bytes=256)
             return codes[key], scales[key]
 
-        def Q(u):
+        def Q(u, lo=0, hi=CHUNK):
             name, c, g = u
             if name == "w":
                 cd, sc = planes(u, CHUNK)
-                cols = slice(0, CHUNK)
+                cols = slice(lo, hi)
             else:
                 cd, sc = planes(("x", c // 2, g), T_TILE)
-                cols = slice((c % 2) * CHUNK, (c % 2 + 1) * CHUNK)
-            nc.vector.quantize_mx(out=cd[:, cols].bitcast(FP8X4), scales=sc[:, cols], in_=grouped[u][:])
+                cols = slice((c % 2) * CHUNK + lo, (c % 2) * CHUNK + hi)
+            nc.vector.quantize_mx(
+                out=cd[:, cols].bitcast(FP8X4), scales=sc[:, cols], in_=grouped[u][:, PACK * lo : PACK * hi]
+            )
 
         def DQ(i, g):
             cols = slice((i % 2) * P, (i % 2 + 1) * P)
@@ -112,9 +106,11 @@ def tile_mix_tierw_relu2_kernel(tc, w, x, out):
             )
             free_banks.append(bank_of["d", i, g])
 
-        def QR(c, g):
+        def QR(c, g, lo=0, hi=CHUNK):
             cd, sc = planes(("r", c, g), CHUNK)
-            nc.vector.quantize_mx(out=cd[:].bitcast(FP8X4), scales=sc[:], in_=resid[c, g][:])
+            nc.vector.quantize_mx(
+                out=cd[:, lo:hi].bitcast(FP8X4), scales=sc[:, lo:hi], in_=resid[c, g][:, PACK * lo : PACK * hi]
+            )
 
         def MM(i, tt, g, tier, lo=0, hi=T_TILE):
             t = (tt, lo)
@@ -160,12 +156,11 @@ def tile_mix_tierw_relu2_kernel(tc, w, x, out):
 
         def IDENT():
             ramp = keep.tile([P, K_PASS + PACK], BF16, name="ramp")
-            nc.gpsimd.memset(ramp[:], 0.0)
+            nc.vector.memset(ramp[:], 0.0)
             nc.gpsimd.affine_select(
                 out=ramp[:], in_=ramp[:], compare_op=ALU.not_equal, fill=1.0,
                 base=PACK - 1, pattern=[[-1, K_PASS + PACK]], channel_multiplier=PACK,
             )
-            ident = keep.tile([P, PACK * K_PASS], BF16, name="ident", align_bytes=64)
             for j in range(PACK):
                 dst = ident[:, j * K_PASS : (j + 1) * K_PASS]
                 src = ramp[:, PACK - 1 - j : PACK - 1 - j + K_PASS]
@@ -173,15 +168,20 @@ def tile_mix_tierw_relu2_kernel(tc, w, x, out):
                     nc.scalar.activation(out=dst, in_=src, func=ACT.Square)
                 else:
                     nc.vector.tensor_copy(out=dst, in_=src)
+
+        def QI():
             nc.vector.quantize_mx(out=id_codes[:].bitcast(FP8X4), scales=id_scales[:], in_=ident[:])
 
+        ident = keep.tile([P, PACK * K_PASS], BF16, name="ident", align_bytes=64)
         id_codes = keep.tile([P, K_PASS], U32, name="id_codes", align_bytes=256)
         id_scales = keep.tile([P, K_PASS], U8, name="id_scales", align_bytes=256)
 
 
-        WA = [("w", 0, 0), ("w", 1, 0), ("w", 0, 1), ("w", 1, 1)]
-        WB = [("w", 2, 0), ("w", 2, 1), ("w", 3, 0), ("w", 3, 1)]
-        X = [("x", 2 * t + h, g) for t in range(3) for g in (0, 1) for h in (0, 1)]
+        def W(c, g):
+            return ("w", c, g)
+
+        def X(t, h, g):
+            return ("x", 2 * t + h, g)
 
         def D2(u):
             DQ(2 * u[1], u[2])
@@ -190,8 +190,8 @@ def tile_mix_tierw_relu2_kernel(tc, w, x, out):
         def S1(u, h):
             SUB(2 * u[1] + h, u[2])
 
-        def Q2(u):
-            QR(u[1], u[2])
+        def Q2(u, lo=0, hi=CHUNK):
+            QR(u[1], u[2], lo, hi)
 
         def M(tiles, ts, g, p):
             for i in tiles:
@@ -199,55 +199,57 @@ def tile_mix_tierw_relu2_kernel(tc, w, x, out):
                     MM(i, t, g, p)
 
         A = range(4)
-
-        L(WA[0]); L(WA[1]); L2(WA[2], WA[3]); L2(X[0], X[1]); L2(X[2], X[3]); L2(X[4], X[5]); L2(X[6], X[7]); L2(WB[0], WB[2]); L2(WB[1], WB[3]); L2(X[8], X[9]); L2(X[10], X[11])
-        IDENT()
-        C(WA[0], "V", 0, 160); C(WA[0], "S", 160, 256); Q(WA[0]); D2(WA[0])
-        for u in [WA[1], WA[2], WA[3], X[0], X[2]]:
-            C(u, "S")
-        C(X[3], "S", 128, 256); C(X[4], "S"); C(X[5], "S")
-        S1(WA[0], 0); Q(WA[1]); D2(WA[1]); S1(WA[0], 1); Q2(WA[0]); S1(WA[1], 0); Q(WA[2]); D2(WA[2]); S1(WA[1], 1); C(X[1], "V"); Q(WA[3]); D2(WA[3]); Q(X[1]); Q(X[0]); Q2(WA[1])
+        LD("w", 0, 1, 0); LD("w", 1, 2, 0); LD("w", 0, 2, 1); LD("x", 0, 2, 0); LD("x", 0, 2, 1); LD("x", 2, 4, 0); LD("x", 2, 4, 1)
+        LD("w", 2, 4, 0); LD("w", 2, 4, 1); LD("x", 4, 6, 0); LD("x", 4, 6, 1)
+        IDENT(); QI()
+        C(W(0, 0), "V", 0, 160); C(W(0, 0), "S", 160, 256); Q(W(0, 0)); D2(W(0, 0))
+        C(W(1, 0), "V", 0, 160); C(W(1, 0), "S", 160, 256); Q(W(1, 0)); D2(W(1, 0))
+        S1(W(0, 0), 0); S1(W(0, 0), 1); C(W(0, 1), "S"); C(W(1, 1), "S", 0, 128)
+        S1(W(1, 0), 0); Q2(W(0, 0)); S1(W(1, 0), 1); C(W(1, 1), "V", 128, 256); Q(W(0, 1)); D2(W(0, 1)); Q2(W(1, 0)); Q(W(1, 1)); D2(W(1, 1))
+        C(X(0, 1, 0), "V"); C(X(0, 0, 0), "S"); S1(W(0, 1), 0); Q(X(0, 1, 0)); Q(X(0, 0, 0))
         M(A, (0,), 0, 0); M(A, (0,), 0, 1)
-        S1(WA[2], 0); C(X[3], "V", 0, 128); S1(WA[2], 1); Q(X[2]); Q2(WA[2]); Q(X[3]); S1(WA[3], 0); S1(WA[3], 1); Q(X[4]); Q2(WA[3]); Q(X[5]); C(X[7], "V")
-        M(A, (0,), 1, 0); M(A, (0,), 1, 1)
-        C(X[6], "V"); Q(X[7])
-        for i in A:
-            R(i, 0, "S")
+        S1(W(0, 1), 1); C(X(0, 1, 1), "V"); C(X(0, 0, 1), "S"); Q2(W(0, 1)); Q(X(0, 1, 1)); S1(W(1, 1), 0); Q(X(0, 0, 1))
+        M(A, (0,), 1, 0); M((0, 1), (0,), 1, 1)
+        S1(W(1, 1), 1); C(X(1, 1, 0), "V"); C(X(1, 0, 0), "S"); Q2(W(1, 1)); Q(X(1, 1, 0)); Q(X(1, 0, 0))
+        M((2, 3), (0,), 1, 1)
         for i in A:
             M((i,), (1,), 0, 0); M((i,), (1,), 0, 1)
-        Q(X[6])
-        C(WB[0], "V"); C(WB[2], "S"); Q(WB[0]); Q(WB[2])
+        R(0, 0, "S"); R(1, 0, "S")
+        C(X(1, 1, 1), "V"); C(X(1, 0, 1), "S", 0, 128); C(X(1, 0, 1), "V", 128, 256); Q(X(1, 1, 1)); Q(X(1, 0, 1))
+        R(2, 0, "S"); R(3, 0, "S")
+        SQ(0, 0, "V"); ST(0, 0, 512); SQ(1, 0, "S"); ST(1, 0, 512)
+        C(W(2, 0), "V", 0, 128); C(W(2, 0), "V", 128, 256); C(W(3, 0), "S"); Q(W(2, 0), 0, 128); Q(W(2, 0), 128, 256)
         for i in A:
             M((i,), (1,), 1, 0); M((i,), (1,), 1, 1)
-            if i == 1:
-                D2(WB[0])
+            if i == 0:
+                R(0, 1, "V"); Q(W(3, 0))
             if i == 2:
-                D2(WB[2])
-        S1(WB[0], 0); C(WB[1], "V"); S1(WB[0], 1); Q(WB[1]); Q2(WB[0])
-        for i in A:
-            R(i, 1, "S")
-        C(WB[3], "S")
-        M((4, 5), (0, 1), 0, 0); D2(WB[1]); S1(WB[2], 0); S1(WB[2], 1); S1(WB[1], 0); Q(WB[3]); S1(WB[1], 1); Q2(WB[2]); Q2(WB[1])
-        M((4, 5), (0, 1), 0, 1); M((4,), (0, 1), 1, 0); D2(WB[3]); M((5,), (0, 1), 1, 0); M((4, 5), (0, 1), 1, 1)
-        for i in A:
-            SQ(i, 0, "S", 0, 1024); ST(i, 0, 1024)
-        S1(WB[3], 0); S1(WB[3], 1); C(X[8], "V"); Q2(WB[3]); C(X[9], "V"); Q(X[8]); Q(X[9])
-        C(X[10], "V"); C(X[11], "V"); Q(X[10]); Q(X[11])
-        for i in (4, 5):
-            R(i, 0, "S"); R(i, 1, "S")
-        for i in (6, 7):
-            M((i,), (0, 1), 0, 0); M((i,), (0, 1), 1, 0); M((i,), (0, 1), 0, 1); M((i,), (0, 1), 1, 1)
-        for i in (4, 5):
-            SQ(i, 0, "S", 0, 1024); ST(i, 0, 1024)
-        for i in (6, 7):
-            R(i, 0, "V"); R(i, 1, "V"); SQ(i, 0, "S", 0, 1024); ST(i, 0, 1024)
-
-        for i in range(6):
+                D2(W(2, 0))
+        D2(W(3, 0))
+        R(1, 1, "S"); R(2, 1, "S")
+        S1(W(2, 0), 0); S1(W(2, 0), 1)
+        C(W(2, 1), "S"); R(3, 1, "S"); C(W(3, 1), "S")
+        M((4, 5), (0, 1), 0, 0)
+        Q2(W(2, 0), 0, 128); S1(W(3, 0), 0); Q2(W(2, 0), 128, 256); Q(W(2, 1)); S1(W(3, 0), 1); C(X(2, 0, 0), "V"); Q2(W(3, 0))
+        M((4,), (0, 1), 0, 1); M((5,), (0,), 0, 1); D2(W(2, 1)); M((5,), (1,), 0, 1); M((4, 5), (0, 1), 1, 0)
+        S1(W(2, 1), 0); S1(W(2, 1), 1); Q(W(3, 1)); Q2(W(2, 1)); Q(X(2, 0, 0))
+        M((6,), (0, 1), 0, 0); M((6,), (0,), 0, 1); D2(W(3, 1)); M((4,), (0, 1), 1, 1); M((5,), (0, 1), 1, 1)
+        SQ(2, 0, "S", 0, 1024); ST(2, 0, 1024); SQ(3, 0, "S", 0, 1024); ST(3, 0, 1024)
+        SQ(0, 1, "S"); ST(0, 512, 1024); SQ(1, 1, "S"); ST(1, 512, 1024)
+        S1(W(3, 1), 0); S1(W(3, 1), 1); C(X(2, 1, 0), "V"); Q2(W(3, 1))
+        M((6,), (1,), 0, 1); M((6,), (0, 1), 1, 0)
+        M((7,), (0, 1), 0, 0); M((6,), (0, 1), 1, 1)
+        R(4, 0, "S"); R(4, 1, "S")
+        M((7,), (0, 1), 0, 1); M((7,), (0, 1), 1, 0); M((7,), (0, 1), 1, 1)
+        C(X(2, 0, 1), "V"); Q(X(2, 1, 0)); C(X(2, 1, 1), "V"); Q(X(2, 0, 1)); Q(X(2, 1, 1))
+        R(5, 0, "S"); SQ(4, 0, "S", 0, 1024); ST(4, 0, 1024); R(5, 1, "S"); SQ(5, 0, "V", 0, 1024); ST(5, 0, 1024)
+        R(6, 0, "S"); R(6, 1, "S"); SQ(6, 0, "V", 0, 1024); ST(6, 0, 1024)
+        R(7, 0, "S"); R(7, 1, "S"); SQ(7, 0, "V", 0, 1024); ST(7, 0, 1024)
+        for i in range(5):
             for g in (0, 1):
                 M((i,), (2,), g, 0); M((i,), (2,), g, 1)
-            R(i, 2, "V"); SQ(i, 2, "S"); ST(i, 1024, 1536)
-        for i in (6, 7):
-            for lo in (0, 256):
-                for g in (0, 1):
-                    MM(i, 2, g, 0, lo, lo + 256); MM(i, 2, g, 1, lo, lo + 256)
-                R(i, 2, "V", lo, lo + 256); SQ(i, 2, "S", lo, lo + 256); ST(i, 1024 + lo, 1280 + lo)
+            R(i, 2, "S"); SQ(i, 2, "V"); ST(i, 1024, 1536)
+        for i, lo, hi in ((5, 0, 256), (5, 256, 512), (6, 0, 256), (6, 256, 512), (7, 0, 256), (7, 256, 384), (7, 384, 512)):
+            for g in (0, 1):
+                MM(i, 2, g, 0, lo, hi); MM(i, 2, g, 1, lo, hi)
+            R(i, 2, "S", lo, hi); SQ(i, 2, "V", lo, hi); ST(i, 1024 + lo, 1024 + hi)

@@ -97,7 +97,7 @@ def tile_mix_tierw_relu2_kernel(tc, w, x, out):
         def SUB(i, g):
             c, h = divmod(i, 2)
             if (c, g) not in resid:
-                resid[c, g] = stage.tile([P, PACK * CHUNK], BF16, name="resid", bufs=3, align_bytes=64)
+                resid[c, g] = stage.tile([P, PACK * CHUNK], BF16, name="resid", bufs=4, align_bytes=64)
             nc.vector.tensor_tensor(
                 out=by_pairs_words(resid[c, g][:, h * K_PASS : (h + 1) * K_PASS]),
                 in0=by_pairs_rows(raw["w", c, g][:, :, h * P : (h + 1) * P]),
@@ -198,58 +198,84 @@ def tile_mix_tierw_relu2_kernel(tc, w, x, out):
                 for t in ts:
                     MM(i, t, g, p)
 
+        def CW(i, g, eng):
+            C(W(i // 2, g), eng, (i % 2) * P, (i % 2 + 1) * P)
+
+        def QW(i, g):
+            Q(W(i // 2, g), (i % 2) * P, (i % 2 + 1) * P)
+
+        def QL(i, g):
+            QR(i // 2, g, (i % 2) * P, (i % 2 + 1) * P)
+
+        def CX(t, q, g, eng):
+            C(X(t, q // 2, g), eng, (q % 2) * P, (q % 2 + 1) * P)
+
+        def QX(t, h, g):
+            Q(X(t, h, g))
+
+        def MT(i, t):
+            for g in (0, 1):
+                MM(i, t, g, 0); MM(i, t, g, 1)
+
         A = range(4)
-        LD("w", 0, 1, 0); LD("w", 1, 2, 0); LD("w", 0, 2, 1); LD("x", 0, 2, 0); LD("x", 0, 2, 1); LD("x", 2, 4, 0); LD("x", 2, 4, 1)
+        LD("w", 0, 2, 0); LD("w", 0, 2, 1); LD("x", 0, 2, 0); LD("x", 0, 2, 1); LD("x", 2, 4, 0); LD("x", 2, 4, 1)
         LD("w", 2, 4, 0); LD("w", 2, 4, 1); LD("x", 4, 6, 0); LD("x", 4, 6, 1)
         IDENT(); QI()
-        C(W(0, 0), "V", 0, 160); C(W(0, 0), "S", 160, 256); Q(W(0, 0)); D2(W(0, 0))
-        C(W(1, 0), "V", 0, 160); C(W(1, 0), "S", 160, 256); Q(W(1, 0)); D2(W(1, 0))
-        S1(W(0, 0), 0); S1(W(0, 0), 1); C(W(0, 1), "S"); C(W(1, 1), "S", 0, 128)
-        S1(W(1, 0), 0); Q2(W(0, 0)); S1(W(1, 0), 1); C(W(1, 1), "V", 128, 256); Q(W(0, 1)); D2(W(0, 1)); Q2(W(1, 0)); Q(W(1, 1)); D2(W(1, 1))
-        C(X(0, 1, 0), "V"); C(X(0, 0, 0), "S"); S1(W(0, 1), 0); Q(X(0, 1, 0)); Q(X(0, 0, 0))
+        CW(0, 0, "V"); CW(1, 0, "S"); CW(2, 0, "V"); QW(0, 0); DQ(0, 0); QW(1, 0); DQ(1, 0); CW(3, 0, "V"); QW(2, 0); DQ(2, 0)
+        for i in A:
+            CW(i, 1, "S")
+        SUB(0, 0); QW(3, 0); DQ(3, 0); SUB(1, 0); QW(0, 1); DQ(0, 1); SUB(2, 0); QW(1, 1); DQ(1, 1); Q2(W(0, 0)); SUB(3, 0); QW(2, 1); QW(3, 1); DQ(2, 1); DQ(3, 1)
+        for q in range(3):
+            CX(0, q, 0, "S")
+        CX(0, 3, 0, "V"); Q2(W(1, 0)); QX(0, 0, 0); QX(0, 1, 0); SUB(0, 1)
         M(A, (0,), 0, 0); M(A, (0,), 0, 1)
-        S1(W(0, 1), 1); C(X(0, 1, 1), "V"); C(X(0, 0, 1), "S"); Q2(W(0, 1)); Q(X(0, 1, 1)); S1(W(1, 1), 0); Q(X(0, 0, 1))
+        for q in A:
+            CX(0, q, 1, "S")
+        SUB(1, 1); QX(0, 0, 1); SUB(2, 1); QX(0, 1, 1); Q2(W(0, 1)); SUB(3, 1)
         M(A, (0,), 1, 0); M((0, 1), (0,), 1, 1)
-        S1(W(1, 1), 1); C(X(1, 1, 0), "V"); C(X(1, 0, 0), "S"); Q2(W(1, 1)); Q(X(1, 1, 0)); Q(X(1, 0, 0))
+        for q in range(3):
+            CX(1, q, 0, "S")
+        CX(1, 3, 0, "V"); Q2(W(1, 1)); QX(1, 0, 0); QX(1, 1, 0)
         M((2, 3), (0,), 1, 1)
         for i in A:
             M((i,), (1,), 0, 0); M((i,), (1,), 0, 1)
-        R(0, 0, "S"); R(1, 0, "S")
-        C(X(1, 1, 1), "V"); C(X(1, 0, 1), "S", 0, 128); C(X(1, 0, 1), "V", 128, 256); Q(X(1, 1, 1)); Q(X(1, 0, 1))
-        R(2, 0, "S"); R(3, 0, "S")
-        SQ(0, 0, "V"); ST(0, 0, 512); SQ(1, 0, "S"); ST(1, 0, 512)
-        C(W(2, 0), "V", 0, 128); C(W(2, 0), "V", 128, 256); C(W(3, 0), "S"); Q(W(2, 0), 0, 128); Q(W(2, 0), 128, 256)
+        R(0, 0, "S"); CX(1, 3, 1, "S")
+        CX(1, 0, 1, "V"); CX(1, 1, 1, "V"); CX(1, 2, 1, "V"); QX(1, 0, 1); QX(1, 1, 1)
+        R(1, 0, "S"); SQ(0, 0, "V"); R(2, 0, "V"); SQ(1, 0, "S"); R(3, 0, "S")
+        CW(4, 0, "V"); CW(5, 0, "S"); CW(6, 0, "V"); QW(4, 0); QW(5, 0); CW(7, 0, "V"); QW(6, 0)
         for i in A:
             M((i,), (1,), 1, 0); M((i,), (1,), 1, 1)
-            if i == 0:
-                R(0, 1, "V"); Q(W(3, 0))
             if i == 2:
-                D2(W(2, 0))
-        D2(W(3, 0))
-        R(1, 1, "S"); R(2, 1, "S")
-        S1(W(2, 0), 0); S1(W(2, 0), 1)
-        C(W(2, 1), "S"); R(3, 1, "S"); C(W(3, 1), "S")
-        M((4, 5), (0, 1), 0, 0)
-        Q2(W(2, 0), 0, 128); S1(W(3, 0), 0); Q2(W(2, 0), 128, 256); Q(W(2, 1)); S1(W(3, 0), 1); C(X(2, 0, 0), "V"); Q2(W(3, 0))
-        M((4,), (0, 1), 0, 1); M((5,), (0,), 0, 1); D2(W(2, 1)); M((5,), (1,), 0, 1); M((4, 5), (0, 1), 1, 0)
-        S1(W(2, 1), 0); S1(W(2, 1), 1); Q(W(3, 1)); Q2(W(2, 1)); Q(X(2, 0, 0))
-        M((6,), (0, 1), 0, 0); M((6,), (0,), 0, 1); D2(W(3, 1)); M((4,), (0, 1), 1, 1); M((5,), (0, 1), 1, 1)
-        SQ(2, 0, "S", 0, 1024); ST(2, 0, 1024); SQ(3, 0, "S", 0, 1024); ST(3, 0, 1024)
-        SQ(0, 1, "S"); ST(0, 512, 1024); SQ(1, 1, "S"); ST(1, 512, 1024)
-        S1(W(3, 1), 0); S1(W(3, 1), 1); C(X(2, 1, 0), "V"); Q2(W(3, 1))
-        M((6,), (1,), 0, 1); M((6,), (0, 1), 1, 0)
-        M((7,), (0, 1), 0, 0); M((6,), (0, 1), 1, 1)
-        R(4, 0, "S"); R(4, 1, "S")
-        M((7,), (0, 1), 0, 1); M((7,), (0, 1), 1, 0); M((7,), (0, 1), 1, 1)
-        C(X(2, 0, 1), "V"); Q(X(2, 1, 0)); C(X(2, 1, 1), "V"); Q(X(2, 0, 1)); Q(X(2, 1, 1))
-        R(5, 0, "S"); SQ(4, 0, "S", 0, 1024); ST(4, 0, 1024); R(5, 1, "S"); SQ(5, 0, "V", 0, 1024); ST(5, 0, 1024)
-        R(6, 0, "S"); R(6, 1, "S"); SQ(6, 0, "V", 0, 1024); ST(6, 0, 1024)
-        R(7, 0, "S"); R(7, 1, "S"); SQ(7, 0, "V", 0, 1024); ST(7, 0, 1024)
-        for i in range(5):
-            for g in (0, 1):
-                M((i,), (2,), g, 0); M((i,), (2,), g, 1)
-            R(i, 2, "S"); SQ(i, 2, "V"); ST(i, 1024, 1536)
+                DQ(4, 0)
+        DQ(5, 0)
+        for i in A:
+            R(i, 1, "S")
+        SUB(4, 0); SUB(5, 0)
+        M((4, 5), (0, 1), 0, 0); DQ(6, 0); M((6,), (0, 1), 0, 0)
+        CW(4, 1, "S"); CW(5, 1, "S"); CW(6, 1, "S")
+        QL(4, 0); CW(7, 1, "V"); QL(5, 0); QW(4, 1); SUB(6, 0)
+        M((4,), (0, 1), 0, 1); DQ(4, 1); M((5,), (0, 1), 0, 1)
+        QW(5, 1); QW(6, 1); QL(6, 0); SUB(4, 1)
+        DQ(5, 1); M((4,), (0, 1), 1, 0); M((6,), (0, 1), 0, 1)
+        SQ(0, 1, "S"); ST(0, 0, 1024); SQ(1, 1, "S"); ST(1, 0, 1024); CX(2, 0, 0, "S")
+        SUB(5, 1); DQ(6, 1); M((5,), (0, 1), 1, 0); M((6,), (0, 1), 1, 0)
+        QL(4, 1); CX(2, 2, 0, "V"); QL(5, 1); SUB(6, 1); CX(2, 3, 0, "V"); QL(6, 1); QW(7, 0); QW(7, 1)
+        SQ(2, 0, "S", 0, 1024); ST(2, 0, 1024); CX(2, 1, 0, "S"); SQ(3, 0, "S", 0, 1024); ST(3, 0, 1024)
+        M((4, 5, 6), (0, 1), 1, 1); DQ(7, 0); DQ(7, 1)
+        QX(2, 0, 0); QX(2, 1, 0); C(X(2, 0, 1), "V"); C(X(2, 1, 1), "V"); QX(2, 0, 1); QX(2, 1, 1)
+        R(4, 0, "S"); R(4, 1, "S"); R(5, 0, "S")
+        M((0, 1, 2), (2,), 0, 0); M((0, 1, 2), (2,), 0, 1)
+        SQ(4, 0, "S", 0, 1024); ST(4, 0, 1024); R(5, 1, "S"); R(6, 0, "S"); R(6, 1, "V"); SQ(5, 0, "S", 0, 1024); ST(5, 0, 1024)
+        SUB(7, 0); SUB(7, 1)
+        for i in (0, 1, 2):
+            M((i,), (2,), 1, 0); M((i,), (2,), 1, 1)
+        SQ(6, 0, "S", 0, 1024); ST(6, 0, 1024)
+        QL(7, 0); R(0, 2, "V"); QL(7, 1); SQ(0, 2, "S"); ST(0, 1024, 1536)
+        for i in (1, 2):
+            R(i, 2, "V"); SQ(i, 2, "S"); ST(i, 1024, 1536)
+        for i, t in ((3, 2), (4, 2), (7, 0), (7, 1)):
+            MT(i, t); R(i, t, "V"); SQ(i, t, "S"); ST(i, 512 * t, 512 * t + 512)
         for i, lo, hi in ((5, 0, 256), (5, 256, 512), (6, 0, 256), (6, 256, 512), (7, 0, 256), (7, 256, 384), (7, 384, 512)):
             for g in (0, 1):
                 MM(i, 2, g, 0, lo, hi); MM(i, 2, g, 1, lo, hi)
-            R(i, 2, "S", lo, hi); SQ(i, 2, "V", lo, hi); ST(i, 1024 + lo, 1024 + hi)
+            R(i, 2, "V", lo, hi); SQ(i, 2, "S", lo, hi); ST(i, 1024 + lo, 1024 + hi)

@@ -33,7 +33,7 @@ def tile_mix_tierw_relu2_kernel(tc, w, x, out):
         ctx.enter_context(tc.manual_schedule())
 
         raw, grouped, codes, scales = {}, {}, {}, {}
-        deq, resid, acc, res = {}, {}, {}, {}
+        deq, resid, acc, res, fourth = {}, {}, {}, {}, {}
 
         def by_pairs_rows(ap):
             return ap.rearrange("p t (c i) -> p c t i", i=PAIR)
@@ -60,6 +60,27 @@ def tile_mix_tierw_relu2_kernel(tc, w, x, out):
                 nc.gpsimd.tensor_scalar(out=dst, in0=src, scalar1=1.0, scalar2=0.0, op0=ALU.mult, op1=ALU.add)
             else:
                 nc.scalar.copy(out=dst, in_=src)
+
+        def C4(u, eng):
+            fourth[u] = keep.tile([P, PACK * P], BF16, name="fourth", align_bytes=64)
+            dst = by_pairs_words(fourth[u][:])
+            src = by_pairs_rows(raw[u][:, :, P:CHUNK])
+            if eng == "V":
+                nc.vector.tensor_copy(out=dst, in_=src)
+            elif eng == "S":
+                nc.scalar.copy(out=dst, in_=src)
+            else:
+                nc.gpsimd.tensor_scalar(out=dst, in0=src, scalar1=1.0, scalar2=0.0, op0=ALU.mult, op1=ALU.add)
+
+        def Q4(u):
+            name, c, g = u
+            if name == "w":
+                cd, sc = planes(u, CHUNK)
+                cols = slice(P, CHUNK)
+            else:
+                cd, sc = planes(("x", c // 2, g), T_TILE)
+                cols = slice(T_TILE - P, T_TILE)
+            nc.vector.quantize_mx(out=cd[:, cols].bitcast(FP8X4), scales=sc[:, cols], in_=fourth[u][:])
 
         def planes(key, width):
             if key not in codes:
@@ -90,6 +111,19 @@ def tile_mix_tierw_relu2_kernel(tc, w, x, out):
                     lhsT_scale=id_scales[:, j * P : (j + 1) * P],
                     rhs=codes["w", i // 2, g][:, cols].bitcast(FP8X4),
                     rhs_scale=scales["w", i // 2, g][:, cols],
+                    start=True,
+                    stop=True,
+                )
+
+        def WARM(count, b):
+            bank = psum.tile([P, T_TILE], F32, name="bank_%d" % b)
+            for r in range(count):
+                nc.tensor.matmul_mx(
+                    out=bank[:],
+                    lhsT=id_codes[:, 0:P].bitcast(FP8X4),
+                    lhsT_scale=id_scales[:, 0:P],
+                    rhs=id_codes[:].bitcast(FP8X4),
+                    rhs_scale=id_scales[:],
                     start=True,
                     stop=True,
                 )
@@ -221,28 +255,24 @@ def tile_mix_tierw_relu2_kernel(tc, w, x, out):
         LD("w", 0, 2, 0); LD("w", 0, 2, 1); LD("x", 0, 2, 0); LD("x", 0, 2, 1); LD("x", 2, 4, 0); LD("x", 2, 4, 1)
         LD("w", 2, 4, 0); LD("w", 2, 4, 1); LD("x", 4, 6, 0); LD("x", 4, 6, 1)
         IDENT(); QI()
-        CW(0, 0, "V"); CW(1, 0, "S"); CW(2, 0, "V"); QW(0, 0); DQ(0, 0); QW(1, 0); DQ(1, 0); CW(3, 0, "V"); QW(2, 0); DQ(2, 0)
-        for i in A:
-            CW(i, 1, "S")
-        SUB(0, 0); QW(3, 0); DQ(3, 0); SUB(1, 0); QW(0, 1); DQ(0, 1); SUB(2, 0); QW(1, 1); DQ(1, 1); Q2(W(0, 0)); SUB(3, 0); QW(2, 1); QW(3, 1); DQ(2, 1); DQ(3, 1)
-        for q in range(3):
-            CX(0, q, 0, "S")
-        CX(0, 3, 0, "V"); Q2(W(1, 0)); QX(0, 0, 0); QX(0, 1, 0); SUB(0, 1)
+        WARM(4, 7)
+        CW(0, 0, "V"); CW(1, 0, "S"); CW(2, 0, "V"); C4(W(1, 0), "S"); QW(0, 0); DQ(0, 0); QW(1, 0); DQ(1, 0); QW(2, 0); DQ(2, 0); Q4(W(1, 0)); DQ(3, 0)
+        C4(W(1, 1), "G"); C(W(0, 1), "S"); CW(2, 1, "S")
+        SUB(0, 0); SUB(1, 0); SUB(2, 0); Q(W(0, 1)); D2(W(0, 1)); Q2(W(0, 0)); QW(2, 1); Q4(W(1, 1)); D2(W(1, 1)); WARM(2, free_banks[0])
+        C4(X(0, 1, 0), "G"); C(X(0, 0, 0), "S"); CX(0, 2, 0, "S")
+        SUB(3, 0); SUB(0, 1); QX(0, 0, 0); Q2(W(1, 0)); Q(X(0, 1, 0), 0, P); Q4(X(0, 1, 0))
         M(A, (0,), 0, 0); M(A, (0,), 0, 1)
-        for q in A:
-            CX(0, q, 1, "S")
-        SUB(1, 1); QX(0, 0, 1); SUB(2, 1); QX(0, 1, 1); Q2(W(0, 1)); SUB(3, 1)
+        C4(X(0, 1, 1), "G"); C(X(0, 0, 1), "S"); CX(0, 2, 1, "S")
+        SUB(1, 1); SUB(2, 1); QX(0, 0, 1); Q2(W(0, 1)); Q(X(0, 1, 1), 0, P); Q4(X(0, 1, 1))
         M(A, (0,), 1, 0); M((0, 1), (0,), 1, 1)
-        for q in range(3):
-            CX(1, q, 0, "S")
-        CX(1, 3, 0, "V"); Q2(W(1, 1)); QX(1, 0, 0); QX(1, 1, 0)
+        C(X(1, 0, 0), "S"); CX(1, 2, 0, "S"); SUB(3, 1); CX(1, 3, 0, "V"); Q2(W(1, 1)); QX(1, 0, 0); QX(1, 1, 0)
         M((2, 3), (0,), 1, 1)
         for i in A:
             M((i,), (1,), 0, 0); M((i,), (1,), 0, 1)
         R(0, 0, "S"); CX(1, 3, 1, "S")
-        CX(1, 0, 1, "V"); CX(1, 1, 1, "V"); CX(1, 2, 1, "V"); QX(1, 0, 1); QX(1, 1, 1)
-        R(1, 0, "S"); SQ(0, 0, "V"); R(2, 0, "V"); SQ(1, 0, "S"); R(3, 0, "S")
-        CW(4, 0, "V"); CW(5, 0, "S"); CW(6, 0, "V"); QW(4, 0); QW(5, 0); CW(7, 0, "V"); QW(6, 0)
+        C(X(1, 0, 1), "V"); CX(1, 2, 1, "V"); QX(1, 0, 1); QX(1, 1, 1)
+        R(1, 0, "S"); R(2, 0, "V"); SQ(0, 0, "S"); R(3, 0, "S")
+        CW(4, 0, "V"); CW(5, 0, "S"); CW(6, 0, "V"); QW(4, 0); CW(7, 0, "V"); QW(5, 0); QW(6, 0); SQ(1, 0, "V")
         for i in A:
             M((i,), (1,), 1, 0); M((i,), (1,), 1, 1)
             if i == 2:
@@ -252,7 +282,7 @@ def tile_mix_tierw_relu2_kernel(tc, w, x, out):
             R(i, 1, "S")
         SUB(4, 0); SUB(5, 0)
         M((4, 5), (0, 1), 0, 0); DQ(6, 0); M((6,), (0, 1), 0, 0)
-        CW(4, 1, "S"); CW(5, 1, "S"); CW(6, 1, "S")
+        C(W(2, 1), "S"); CW(6, 1, "S")
         QL(4, 0); CW(7, 1, "V"); QL(5, 0); QW(4, 1); SUB(6, 0)
         M((4,), (0, 1), 0, 1); DQ(4, 1); M((5,), (0, 1), 0, 1)
         QW(5, 1); QW(6, 1); QL(6, 0); SUB(4, 1)
@@ -274,8 +304,8 @@ def tile_mix_tierw_relu2_kernel(tc, w, x, out):
         for i in (1, 2):
             R(i, 2, "V"); SQ(i, 2, "S"); ST(i, 1024, 1536)
         for i, t in ((3, 2), (4, 2), (7, 0), (7, 1)):
-            MT(i, t); R(i, t, "V"); SQ(i, t, "S"); ST(i, 512 * t, 512 * t + 512)
+            MT(i, t); R(i, t, "S"); SQ(i, t, "V"); ST(i, 512 * t, 512 * t + 512)
         for i, lo, hi in ((5, 0, 256), (5, 256, 512), (6, 0, 256), (6, 256, 512), (7, 0, 256), (7, 256, 384), (7, 384, 512)):
             for g in (0, 1):
                 MM(i, 2, g, 0, lo, hi); MM(i, 2, g, 1, lo, hi)
-            R(i, 2, "V", lo, hi); SQ(i, 2, "S", lo, hi); ST(i, 1024 + lo, 1024 + hi)
+            R(i, 2, "S", lo, hi); SQ(i, 2, "V", lo, hi); ST(i, 1024 + lo, 1024 + hi)

@@ -19,6 +19,7 @@ K_PASS = P * PACK
 PASSES = K // K_PASS
 CHUNK = 256
 T_TILE = 512
+W_PLANE_ROW = 4
 PAIR = 4
 
 
@@ -85,7 +86,8 @@ def tile_mix_tierw_relu2_kernel(tc, w, x, out):
         def planes(key, width):
             if key not in codes:
                 codes[key] = keep.tile([P, width], U32, name="codes_%s_%d_%d" % key, align_bytes=256)
-                scales[key] = keep.tile([P, width], U8, name="scales_%s_%d_%d" % key, align_bytes=256)
+                plane = keep.tile([P, width], U8, name="scales_%s_%d_%d" % key, align_bytes=256)
+                scales[key] = plane[(0 if key[0] == "x" else W_PLANE_ROW) : P, :]
             return codes[key], scales[key]
 
         def Q(u, lo=0, hi=CHUNK):
@@ -255,15 +257,13 @@ def tile_mix_tierw_relu2_kernel(tc, w, x, out):
         LD("w", 0, 2, 0); LD("w", 0, 2, 1); LD("x", 0, 2, 0); LD("x", 0, 2, 1); LD("x", 2, 4, 0); LD("x", 2, 4, 1)
         LD("w", 2, 4, 0); LD("w", 2, 4, 1); LD("x", 4, 6, 0); LD("x", 4, 6, 1)
         IDENT(); QI()
-        WARM(4, 7)
-        CW(0, 0, "V"); CW(1, 0, "S"); CW(2, 0, "V"); C4(W(1, 0), "S"); QW(0, 0); DQ(0, 0); QW(1, 0); DQ(1, 0); QW(2, 0); DQ(2, 0); Q4(W(1, 0)); DQ(3, 0)
-        C4(W(1, 1), "G"); C(W(0, 1), "S"); CW(2, 1, "S")
-        SUB(0, 0); SUB(1, 0); SUB(2, 0); Q(W(0, 1)); D2(W(0, 1)); Q2(W(0, 0)); QW(2, 1); Q4(W(1, 1)); D2(W(1, 1)); WARM(2, free_banks[0])
-        C4(X(0, 1, 0), "G"); C(X(0, 0, 0), "S"); CX(0, 2, 0, "S")
-        SUB(3, 0); SUB(0, 1); QX(0, 0, 0); Q2(W(1, 0)); Q(X(0, 1, 0), 0, P); Q4(X(0, 1, 0))
+        WARM(3, 7)
+        CW(0, 0, "V"); CW(1, 0, "S"); CW(2, 0, "V"); CW(3, 0, "S"); QW(0, 0); DQ(0, 0); QW(1, 0); DQ(1, 0); QW(2, 0); DQ(2, 0); QW(3, 0); DQ(3, 0)
+        C(W(0, 1), "S"); C(W(1, 1), "S")
+        SUB(0, 0); SUB(1, 0); SUB(2, 0); Q(W(0, 1)); D2(W(0, 1)); Q2(W(0, 0)); SUB(3, 0); Q(W(1, 1)); D2(W(1, 1)); WARM(2, free_banks[0])
+        C(X(0, 0, 0), "S"); CX(0, 2, 0, "S"); CX(0, 3, 0, "V"); Q2(W(1, 0)); QX(0, 0, 0); SUB(0, 1); QX(0, 1, 0)
         M(A, (0,), 0, 0); M(A, (0,), 0, 1)
-        C4(X(0, 1, 1), "G"); C(X(0, 0, 1), "S"); CX(0, 2, 1, "S")
-        SUB(1, 1); SUB(2, 1); QX(0, 0, 1); Q2(W(0, 1)); Q(X(0, 1, 1), 0, P); Q4(X(0, 1, 1))
+        C(X(0, 0, 1), "S"); CX(0, 2, 1, "S"); SUB(1, 1); CX(0, 3, 1, "V"); QX(0, 0, 1); Q2(W(0, 1)); QX(0, 1, 1); SUB(2, 1)
         M(A, (0,), 1, 0); M((0, 1), (0,), 1, 1)
         C(X(1, 0, 0), "S"); CX(1, 2, 0, "S"); SUB(3, 1); CX(1, 3, 0, "V"); Q2(W(1, 1)); QX(1, 0, 0); QX(1, 1, 0)
         M((2, 3), (0,), 1, 1)
@@ -282,8 +282,8 @@ def tile_mix_tierw_relu2_kernel(tc, w, x, out):
             R(i, 1, "S")
         SUB(4, 0); SUB(5, 0)
         M((4, 5), (0, 1), 0, 0); DQ(6, 0); M((6,), (0, 1), 0, 0)
-        C(W(2, 1), "S"); CW(6, 1, "S")
-        QL(4, 0); CW(7, 1, "V"); QL(5, 0); QW(4, 1); SUB(6, 0)
+        CW(5, 1, "S"); C(W(3, 1), "S")
+        CW(4, 1, "V"); QL(4, 0); QL(5, 0); QW(4, 1); SUB(6, 0)
         M((4,), (0, 1), 0, 1); DQ(4, 1); M((5,), (0, 1), 0, 1)
         QW(5, 1); QW(6, 1); QL(6, 0); SUB(4, 1)
         DQ(5, 1); M((4,), (0, 1), 1, 0); M((6,), (0, 1), 0, 1)
@@ -295,7 +295,7 @@ def tile_mix_tierw_relu2_kernel(tc, w, x, out):
         QX(2, 0, 0); QX(2, 1, 0); C(X(2, 0, 1), "V"); C(X(2, 1, 1), "V"); QX(2, 0, 1); QX(2, 1, 1)
         R(4, 0, "S"); R(4, 1, "S"); R(5, 0, "S")
         M((0, 1, 2), (2,), 0, 0); M((0, 1, 2), (2,), 0, 1)
-        SQ(4, 0, "S", 0, 1024); ST(4, 0, 1024); R(5, 1, "S"); R(6, 0, "S"); R(6, 1, "V"); SQ(5, 0, "S", 0, 1024); ST(5, 0, 1024)
+        SQ(4, 0, "S", 0, 1024); ST(4, 0, 1024); R(5, 1, "S"); R(6, 0, "V"); SQ(5, 0, "S", 0, 1024); ST(5, 0, 1024); R(6, 1, "V")
         SUB(7, 0); SUB(7, 1)
         for i in (0, 1, 2):
             M((i,), (2,), 1, 0); M((i,), (2,), 1, 1)
@@ -303,7 +303,9 @@ def tile_mix_tierw_relu2_kernel(tc, w, x, out):
         QL(7, 0); R(0, 2, "V"); QL(7, 1); SQ(0, 2, "S"); ST(0, 1024, 1536)
         for i in (1, 2):
             R(i, 2, "V"); SQ(i, 2, "S"); ST(i, 1024, 1536)
-        for i, t in ((3, 2), (4, 2), (7, 0), (7, 1)):
+        for i, t in ((3, 2), (4, 2)):
+            MT(i, t); R(i, t, "V"); SQ(i, t, "S"); ST(i, 512 * t, 512 * t + 512)
+        for i, t in ((7, 0), (7, 1)):
             MT(i, t); R(i, t, "S"); SQ(i, t, "V"); ST(i, 512 * t, 512 * t + 512)
         for i, lo, hi in ((5, 0, 256), (5, 256, 512), (6, 0, 256), (6, 256, 512), (7, 0, 256), (7, 256, 384), (7, 384, 512)):
             for g in (0, 1):

@@ -17,297 +17,346 @@ P = 128
 PACK = 4
 K_PASS = P * PACK
 PASSES = K // K_PASS
-CHUNK = 256
-T_TILE = 512
-W_PLANE_ROW = 4
-PAIR = 4
+TIERS = 2
+CHUNK = 512
+UNIT = 256
+RUN = 4
+BANKS = 8
+ROUNDED_BUFS = 8
+REST_BUFS = 4
 
 
 def tile_mix_tierw_relu2_kernel(tc, w, x, out):
     nc = tc.nc
     with ExitStack() as ctx:
         keep = ctx.enter_context(tc.tile_pool(name="keep", bufs=1))
-        stage = ctx.enter_context(tc.tile_pool(name="stage", bufs=8))
+        stage = ctx.enter_context(tc.tile_pool(name="stage", bufs=ROUNDED_BUFS))
         psum = ctx.enter_context(tc.psum_pool(name="psum", bufs=1))
-        free_banks = list(range(8))
-        bank_of = {}
         ctx.enter_context(tc.manual_schedule())
 
-        raw, grouped, codes, scales = {}, {}, {}, {}
-        deq, resid, acc, res, fourth = {}, {}, {}, {}, {}
+        free_banks = list(range(BANKS))
+        bank_of = {}
+        raw, rounded, rest, codes, scales = {}, {}, {}, {}, {}
+        expanded, sums, passes_done, result = {}, {}, {}, {}
 
-        def by_pairs_rows(ap):
-            return ap.rearrange("p t (c i) -> p c t i", i=PAIR)
+        def rows_view(ap):
+            return ap.rearrange("p j (c i) -> p c j i", i=RUN)
 
-        def by_pairs_words(ap):
-            return ap.rearrange("p (c i t) -> p c t i", i=PAIR, t=PACK)
+        def words_view(ap):
+            return ap.rearrange("p (c i j) -> p c j i", i=RUN, j=PACK)
 
-        def LD(name, c0, c1, g):
+        def load(name, panel, g):
             src = w if name == "w" else x
-            panel = keep.tile([P, PACK, (c1 - c0) * CHUNK], F32, name="raw_%s_%d_%d" % (name, c0, g))
-            rows = src[g * K_PASS : (g + 1) * K_PASS, c0 * CHUNK : c1 * CHUNK]
-            nc.sync.dma_start(out=panel[:], in_=rows.rearrange("(p j) n -> p j n", j=PACK))
-            for c in range(c0, c1):
-                raw[name, c, g] = panel[:, :, (c - c0) * CHUNK : (c - c0 + 1) * CHUNK]
+            tile = keep.tile([P, PACK, CHUNK], F32, name="raw_%s_%d_%d" % (name, 2 * panel, g))
+            rows = src[g * K_PASS : (g + 1) * K_PASS, panel * CHUNK : (panel + 1) * CHUNK]
+            nc.sync.dma_start(out=tile[:], in_=rows.rearrange("(p j) n -> p j n", j=PACK))
+            for half in range(2):
+                raw[name, 2 * panel + half, g] = tile[:, :, half * UNIT : (half + 1) * UNIT]
 
-        def C(u, eng, lo=0, hi=CHUNK):
-            if u not in grouped:
-                grouped[u] = stage.tile([P, PACK * CHUNK], BF16, name="grouped", align_bytes=64)
-            dst = by_pairs_words(grouped[u][:, PACK * lo : PACK * hi])
-            src = by_pairs_rows(raw[u][:, :, lo:hi])
-            if eng == "V":
+        def place(first, count):
+            lo = (first % 2) * P
+            return first // 2, lo, lo + count * P
+
+        def round_columns(engine, key, lo, hi):
+            if key not in rounded:
+                rounded[key] = stage.tile([P, PACK * UNIT], BF16, name="grouped", align_bytes=64)
+            dst = words_view(rounded[key][:, PACK * lo : PACK * hi])
+            src = rows_view(raw[key][:, :, lo:hi])
+            if engine is vector:
                 nc.vector.tensor_copy(out=dst, in_=src)
-            elif eng == "G":
-                nc.gpsimd.tensor_scalar(out=dst, in0=src, scalar1=1.0, scalar2=0.0, op0=ALU.mult, op1=ALU.add)
             else:
                 nc.scalar.copy(out=dst, in_=src)
 
-        def C4(u, eng):
-            fourth[u] = keep.tile([P, PACK * P], BF16, name="fourth", align_bytes=64)
-            dst = by_pairs_words(fourth[u][:])
-            src = by_pairs_rows(raw[u][:, :, P:CHUNK])
-            if eng == "V":
-                nc.vector.tensor_copy(out=dst, in_=src)
-            elif eng == "S":
-                nc.scalar.copy(out=dst, in_=src)
-            else:
-                nc.gpsimd.tensor_scalar(out=dst, in0=src, scalar1=1.0, scalar2=0.0, op0=ALU.mult, op1=ALU.add)
+        def round_w(engine, i, g, count=1):
+            unit, lo, hi = place(i, count)
+            round_columns(engine, ("w", unit, g), lo, hi)
 
-        def Q4(u):
-            name, c, g = u
-            if name == "w":
-                cd, sc = planes(u, CHUNK)
-                cols = slice(P, CHUNK)
-            else:
-                cd, sc = planes(("x", c // 2, g), T_TILE)
-                cols = slice(T_TILE - P, T_TILE)
-            nc.vector.quantize_mx(out=cd[:, cols].bitcast(FP8X4), scales=sc[:, cols], in_=fourth[u][:])
+        def round_x(engine, t, q, g, count=1):
+            unit, lo, hi = place(4 * t + q, count)
+            round_columns(engine, ("x", unit, g), lo, hi)
 
-        def planes(key, width):
+        def quantise(key, width, lo, hi, values):
             if key not in codes:
                 codes[key] = keep.tile([P, width], U32, name="codes_%s_%d_%d" % key, align_bytes=256)
-                plane = keep.tile([P, width], U8, name="scales_%s_%d_%d" % key, align_bytes=256)
-                scales[key] = plane[(0 if key[0] == "x" else W_PLANE_ROW) : P, :]
-            return codes[key], scales[key]
+                scales[key] = keep.tile([P, width], U8, name="scales_%s_%d_%d" % key, align_bytes=256)
+            nc.vector.quantize_mx(out=codes[key][:, lo:hi].bitcast(FP8X4), scales=scales[key][:, lo:hi], in_=values)
 
-        def Q(u, lo=0, hi=CHUNK):
-            name, c, g = u
-            if name == "w":
-                cd, sc = planes(u, CHUNK)
-                cols = slice(lo, hi)
-            else:
-                cd, sc = planes(("x", c // 2, g), T_TILE)
-                cols = slice((c % 2) * CHUNK + lo, (c % 2) * CHUNK + hi)
-            nc.vector.quantize_mx(
-                out=cd[:, cols].bitcast(FP8X4), scales=sc[:, cols], in_=grouped[u][:, PACK * lo : PACK * hi]
-            )
+        def quantise_w(i, g, count=1):
+            unit, lo, hi = place(i, count)
+            quantise(("w", unit, g), UNIT, lo, hi, rounded["w", unit, g][:, PACK * lo : PACK * hi])
 
-        def DQ(i, g):
-            cols = slice((i % 2) * P, (i % 2 + 1) * P)
-            bank_of["d", i, g] = free_banks.pop(0)
-            deq[i, g] = psum.tile([P, PACK, P], F32, name="bank_%d" % bank_of["d", i, g])
+        def quantise_rest(i, g, count=1):
+            unit, lo, hi = place(i, count)
+            quantise(("r", unit, g), UNIT, lo, hi, rest[unit, g][:, PACK * lo : PACK * hi])
+
+        def quantise_x(t, half, g):
+            quantise(("x", t, g), CHUNK, half * UNIT, (half + 1) * UNIT, rounded["x", 2 * t + half, g][:])
+
+        def take_bank(key, shape):
+            bank_of[key] = free_banks.pop(0)
+            return psum.tile(shape, F32, name="bank_%d" % bank_of[key])
+
+        def expand(i, g):
+            unit, lo, hi = place(i, 1)
+            expanded[i, g] = take_bank(("expanded", i, g), [P, PACK, P])
             for j in range(PACK):
                 nc.tensor.matmul_mx(
-                    out=deq[i, g][:, j, :],
+                    out=expanded[i, g][:, j, :],
                     lhsT=id_codes[:, j * P : (j + 1) * P].bitcast(FP8X4),
                     lhsT_scale=id_scales[:, j * P : (j + 1) * P],
-                    rhs=codes["w", i // 2, g][:, cols].bitcast(FP8X4),
-                    rhs_scale=scales["w", i // 2, g][:, cols],
+                    rhs=codes["w", unit, g][:, lo:hi].bitcast(FP8X4),
+                    rhs_scale=scales["w", unit, g][:, lo:hi],
                     start=True,
                     stop=True,
                 )
 
-        def WARM(count, b):
-            bank = psum.tile([P, T_TILE], F32, name="bank_%d" % b)
-            for r in range(count):
-                nc.tensor.matmul_mx(
-                    out=bank[:],
-                    lhsT=id_codes[:, 0:P].bitcast(FP8X4),
-                    lhsT_scale=id_scales[:, 0:P],
-                    rhs=id_codes[:].bitcast(FP8X4),
-                    rhs_scale=id_scales[:],
-                    start=True,
-                    stop=True,
-                )
-
-        def SUB(i, g):
-            c, h = divmod(i, 2)
-            if (c, g) not in resid:
-                resid[c, g] = stage.tile([P, PACK * CHUNK], BF16, name="resid", bufs=4, align_bytes=64)
+        def subtract(i, g):
+            unit, lo, hi = place(i, 1)
+            if (unit, g) not in rest:
+                rest[unit, g] = stage.tile([P, PACK * UNIT], BF16, name="resid", bufs=REST_BUFS, align_bytes=64)
             nc.vector.tensor_tensor(
-                out=by_pairs_words(resid[c, g][:, h * K_PASS : (h + 1) * K_PASS]),
-                in0=by_pairs_rows(raw["w", c, g][:, :, h * P : (h + 1) * P]),
-                in1=by_pairs_rows(deq[i, g][:]),
+                out=words_view(rest[unit, g][:, PACK * lo : PACK * hi]),
+                in0=rows_view(raw["w", unit, g][:, :, lo:hi]),
+                in1=rows_view(expanded[i, g][:]),
                 op=ALU.subtract,
             )
-            free_banks.append(bank_of["d", i, g])
+            free_banks.append(bank_of["expanded", i, g])
 
-        def QR(c, g, lo=0, hi=CHUNK):
-            cd, sc = planes(("r", c, g), CHUNK)
-            nc.vector.quantize_mx(
-                out=cd[:, lo:hi].bitcast(FP8X4), scales=sc[:, lo:hi], in_=resid[c, g][:, PACK * lo : PACK * hi]
-            )
-
-        def MM(i, tt, g, tier, lo=0, hi=T_TILE):
-            t = (tt, lo)
-            first = (i, t) not in acc
-            if first:
-                bank_of["a", i, t] = free_banks.pop(0)
-                bank = psum.tile([P, hi - lo], F32, name="bank_%d" % bank_of["a", i, t])
-                acc[i, t] = [bank, 0]
-            acc[i, t][1] = acc[i, t][1] + 1
-            key = ("wr"[tier], i // 2, g)
-            cols = slice((i % 2) * P, (i % 2 + 1) * P)
+        def product(i, t, g, tier, lo=0, hi=CHUNK):
+            key = ("sum", i, t, lo)
+            if key not in sums:
+                sums[key] = take_bank(key, [P, hi - lo])
+                passes_done[key] = 0
+            passes_done[key] = passes_done[key] + 1
+            unit, w_lo, w_hi = place(i, 1)
+            operand = ("wr"[tier], unit, g)
             nc.tensor.matmul_mx(
-                out=acc[i, t][0][:],
-                lhsT=codes[key][:, cols].bitcast(FP8X4),
-                lhsT_scale=scales[key][:, cols],
-                rhs=codes["x", tt, g][:, lo:hi].bitcast(FP8X4),
-                rhs_scale=scales["x", tt, g][:, lo:hi],
-                start=first,
-                stop=acc[i, t][1] == 2 * PASSES,
+                out=sums[key][:],
+                lhsT=codes[operand][:, w_lo:w_hi].bitcast(FP8X4),
+                lhsT_scale=scales[operand][:, w_lo:w_hi],
+                rhs=codes["x", t, g][:, lo:hi].bitcast(FP8X4),
+                rhs_scale=scales["x", t, g][:, lo:hi],
+                start=passes_done[key] == 1,
+                stop=passes_done[key] == TIERS * PASSES,
             )
 
-        def R(i, t, eng, lo=0, hi=T_TILE):
-            if i not in res:
-                res[i] = keep.tile([P, T], F32, name="res_%d" % i)
-            dst = res[i][:, t * T_TILE + lo : t * T_TILE + hi]
-            if eng == "V":
-                nc.vector.tensor_scalar_max(out=dst, in0=acc[i, (t, lo)][0][:], scalar1=0.0)
-            else:
-                nc.scalar.activation(out=dst, in_=acc[i, (t, lo)][0][:], func=ACT.Relu)
-            free_banks.append(bank_of["a", i, (t, lo)])
+        def products(bands, chunks, g, tier):
+            for i in bands:
+                for t in chunks:
+                    product(i, t, g, tier)
 
-        def SQ(i, t, eng, lo=0, hi=T_TILE):
-            dst = res[i][:, t * T_TILE + lo : t * T_TILE + hi]
-            if eng == "V":
+        def both_tiers(i, t, g, lo=0, hi=CHUNK):
+            for tier in range(TIERS):
+                product(i, t, g, tier, lo, hi)
+
+        def relu(engine, i, t, lo=0, hi=CHUNK):
+            if i not in result:
+                result[i] = keep.tile([P, T], F32, name="res_%d" % i)
+            key = ("sum", i, t, lo)
+            dst = result[i][:, t * CHUNK + lo : t * CHUNK + hi]
+            if engine is vector:
+                nc.vector.tensor_scalar_max(out=dst, in0=sums[key][:], scalar1=0.0)
+            else:
+                nc.scalar.activation(out=dst, in_=sums[key][:], func=ACT.Relu)
+            free_banks.append(bank_of[key])
+
+        def square(engine, i, lo, hi):
+            dst = result[i][:, lo:hi]
+            if engine is vector:
                 nc.vector.tensor_tensor(out=dst, in0=dst, in1=dst, op=ALU.mult)
-            elif eng == "G":
-                nc.gpsimd.tensor_tensor(out=dst, in0=dst, in1=dst, op=ALU.mult)
             else:
                 nc.scalar.activation(out=dst, in_=dst, func=ACT.Square)
 
-        def ST(i, lo, hi):
-            nc.sync.dma_start(out=out[i * P : (i + 1) * P, lo:hi], in_=res[i][:, lo:hi])
+        def store(i, lo, hi):
+            nc.sync.dma_start(out=out[i * P : (i + 1) * P, lo:hi], in_=result[i][:, lo:hi])
 
-        def IDENT():
-            ramp = keep.tile([P, K_PASS + PACK], BF16, name="ramp")
-            nc.vector.memset(ramp[:], 0.0)
-            nc.gpsimd.affine_select(
-                out=ramp[:], in_=ramp[:], compare_op=ALU.not_equal, fill=1.0,
-                base=PACK - 1, pattern=[[-1, K_PASS + PACK]], channel_multiplier=PACK,
-            )
-            for j in range(PACK):
-                dst = ident[:, j * K_PASS : (j + 1) * K_PASS]
-                src = ramp[:, PACK - 1 - j : PACK - 1 - j + K_PASS]
-                if j == 0:
-                    nc.scalar.activation(out=dst, in_=src, func=ACT.Square)
-                else:
-                    nc.vector.tensor_copy(out=dst, in_=src)
+        def finish(i, t, lo=0, hi=CHUNK):
+            relu(scalar, i, t, lo, hi)
+            square(vector, i, t * CHUNK + lo, t * CHUNK + hi)
+            store(i, t * CHUNK + lo, t * CHUNK + hi)
 
-        def QI():
-            nc.vector.quantize_mx(out=id_codes[:].bitcast(FP8X4), scales=id_scales[:], in_=ident[:])
-
-        ident = keep.tile([P, PACK * K_PASS], BF16, name="ident", align_bytes=64)
+        vector, scalar = nc.vector, nc.scalar
+        left = range(4)
+        identity = keep.tile([P, PACK * K_PASS], BF16, name="ident", align_bytes=64)
         id_codes = keep.tile([P, K_PASS], U32, name="id_codes", align_bytes=256)
         id_scales = keep.tile([P, K_PASS], U8, name="id_scales", align_bytes=256)
 
+        for name, panel in (("w", 0), ("x", 0), ("x", 1), ("w", 1), ("x", 2)):
+            for g in range(PASSES):
+                load(name, panel, g)
 
-        def W(c, g):
-            return ("w", c, g)
+        one_hot = keep.tile([P, K_PASS + PACK], BF16, name="ramp")
+        nc.vector.memset(one_hot[:], 0.0)
+        nc.gpsimd.affine_select(
+            out=one_hot[:], in_=one_hot[:], compare_op=ALU.not_equal, fill=1.0,
+            base=PACK - 1, pattern=[[-1, K_PASS + PACK]], channel_multiplier=PACK,
+        )
+        for j in range(PACK):
+            dst = identity[:, j * K_PASS : (j + 1) * K_PASS]
+            src = one_hot[:, PACK - 1 - j : PACK - 1 - j + K_PASS]
+            if j == 0:
+                nc.scalar.activation(out=dst, in_=src, func=ACT.Square)
+            else:
+                nc.vector.tensor_copy(out=dst, in_=src)
+        nc.vector.quantize_mx(out=id_codes[:].bitcast(FP8X4), scales=id_scales[:], in_=identity[:])
 
-        def X(t, h, g):
-            return ("x", 2 * t + h, g)
-
-        def D2(u):
-            DQ(2 * u[1], u[2])
-            DQ(2 * u[1] + 1, u[2])
-
-        def S1(u, h):
-            SUB(2 * u[1] + h, u[2])
-
-        def Q2(u, lo=0, hi=CHUNK):
-            QR(u[1], u[2], lo, hi)
-
-        def M(tiles, ts, g, p):
-            for i in tiles:
-                for t in ts:
-                    MM(i, t, g, p)
-
-        def CW(i, g, eng):
-            C(W(i // 2, g), eng, (i % 2) * P, (i % 2 + 1) * P)
-
-        def QW(i, g):
-            Q(W(i // 2, g), (i % 2) * P, (i % 2 + 1) * P)
-
-        def QL(i, g):
-            QR(i // 2, g, (i % 2) * P, (i % 2 + 1) * P)
-
-        def CX(t, q, g, eng):
-            C(X(t, q // 2, g), eng, (q % 2) * P, (q % 2 + 1) * P)
-
-        def QX(t, h, g):
-            Q(X(t, h, g))
-
-        def MT(i, t):
-            for g in (0, 1):
-                MM(i, t, g, 0); MM(i, t, g, 1)
-
-        A = range(4)
-        LD("w", 0, 2, 0); LD("w", 0, 2, 1); LD("x", 0, 2, 0); LD("x", 0, 2, 1); LD("x", 2, 4, 0); LD("x", 2, 4, 1)
-        LD("w", 2, 4, 0); LD("w", 2, 4, 1); LD("x", 4, 6, 0); LD("x", 4, 6, 1)
-        IDENT(); QI()
-        WARM(3, 7)
-        CW(0, 0, "V"); CW(1, 0, "S"); CW(2, 0, "V"); CW(3, 0, "S"); QW(0, 0); DQ(0, 0); QW(1, 0); DQ(1, 0); QW(2, 0); DQ(2, 0); QW(3, 0); DQ(3, 0)
-        C(W(0, 1), "S"); C(W(1, 1), "S")
-        SUB(0, 0); SUB(1, 0); SUB(2, 0); Q(W(0, 1)); D2(W(0, 1)); Q2(W(0, 0)); SUB(3, 0); Q(W(1, 1)); D2(W(1, 1)); WARM(2, free_banks[0])
-        C(X(0, 0, 0), "S"); CX(0, 2, 0, "S"); CX(0, 3, 0, "V"); Q2(W(1, 0)); QX(0, 0, 0); SUB(0, 1); QX(0, 1, 0)
-        M(A, (0,), 0, 0); M(A, (0,), 0, 1)
-        C(X(0, 0, 1), "S"); CX(0, 2, 1, "S"); SUB(1, 1); CX(0, 3, 1, "V"); QX(0, 0, 1); Q2(W(0, 1)); QX(0, 1, 1); SUB(2, 1)
-        M(A, (0,), 1, 0); M((0, 1), (0,), 1, 1)
-        C(X(1, 0, 0), "S"); CX(1, 2, 0, "S"); SUB(3, 1); CX(1, 3, 0, "V"); Q2(W(1, 1)); QX(1, 0, 0); QX(1, 1, 0)
-        M((2, 3), (0,), 1, 1)
-        for i in A:
-            M((i,), (1,), 0, 0); M((i,), (1,), 0, 1)
-        R(0, 0, "S"); CX(1, 3, 1, "S")
-        C(X(1, 0, 1), "V"); CX(1, 2, 1, "V"); QX(1, 0, 1); QX(1, 1, 1)
-        R(1, 0, "S"); R(2, 0, "V"); SQ(0, 0, "S"); R(3, 0, "S")
-        CW(4, 0, "V"); CW(5, 0, "S"); CW(6, 0, "V"); QW(4, 0); CW(7, 0, "V"); QW(5, 0); QW(6, 0); SQ(1, 0, "V")
-        for i in A:
-            M((i,), (1,), 1, 0); M((i,), (1,), 1, 1)
-            if i == 2:
-                DQ(4, 0)
-        DQ(5, 0)
-        for i in A:
-            R(i, 1, "S")
-        SUB(4, 0); SUB(5, 0)
-        M((4, 5), (0, 1), 0, 0); DQ(6, 0); M((6,), (0, 1), 0, 0)
-        CW(5, 1, "S"); C(W(3, 1), "S")
-        CW(4, 1, "V"); QL(4, 0); QL(5, 0); QW(4, 1); SUB(6, 0)
-        M((4,), (0, 1), 0, 1); DQ(4, 1); M((5,), (0, 1), 0, 1)
-        QW(5, 1); QW(6, 1); QL(6, 0); SUB(4, 1)
-        DQ(5, 1); M((4,), (0, 1), 1, 0); M((6,), (0, 1), 0, 1)
-        SQ(0, 1, "S"); ST(0, 0, 1024); SQ(1, 1, "S"); ST(1, 0, 1024); CX(2, 0, 0, "S")
-        SUB(5, 1); DQ(6, 1); M((5,), (0, 1), 1, 0); M((6,), (0, 1), 1, 0)
-        QL(4, 1); CX(2, 2, 0, "V"); QL(5, 1); SUB(6, 1); CX(2, 3, 0, "V"); QL(6, 1); QW(7, 0); QW(7, 1)
-        SQ(2, 0, "S", 0, 1024); ST(2, 0, 1024); CX(2, 1, 0, "S"); SQ(3, 0, "S", 0, 1024); ST(3, 0, 1024)
-        M((4, 5, 6), (0, 1), 1, 1); DQ(7, 0); DQ(7, 1)
-        QX(2, 0, 0); QX(2, 1, 0); C(X(2, 0, 1), "V"); C(X(2, 1, 1), "V"); QX(2, 0, 1); QX(2, 1, 1)
-        R(4, 0, "S"); R(4, 1, "S"); R(5, 0, "S")
-        M((0, 1, 2), (2,), 0, 0); M((0, 1, 2), (2,), 0, 1)
-        SQ(4, 0, "S", 0, 1024); ST(4, 0, 1024); R(5, 1, "S"); R(6, 0, "V"); SQ(5, 0, "S", 0, 1024); ST(5, 0, 1024); R(6, 1, "V")
-        SUB(7, 0); SUB(7, 1)
+        for i in left:
+            round_w(scalar if i % 2 else vector, i, 0)
+        for i in left:
+            quantise_w(i, 0)
+            expand(i, 0)
+        round_w(scalar, 0, 1, count=2)
+        round_w(scalar, 2, 1, count=2)
         for i in (0, 1, 2):
-            M((i,), (2,), 1, 0); M((i,), (2,), 1, 1)
-        SQ(6, 0, "S", 0, 1024); ST(6, 0, 1024)
-        QL(7, 0); R(0, 2, "V"); QL(7, 1); SQ(0, 2, "S"); ST(0, 1024, 1536)
-        for i in (1, 2):
-            R(i, 2, "V"); SQ(i, 2, "S"); ST(i, 1024, 1536)
-        for i, t in ((3, 2), (4, 2)):
-            MT(i, t); R(i, t, "V"); SQ(i, t, "S"); ST(i, 512 * t, 512 * t + 512)
-        for i, t in ((7, 0), (7, 1)):
-            MT(i, t); R(i, t, "S"); SQ(i, t, "V"); ST(i, 512 * t, 512 * t + 512)
-        for i, lo, hi in ((5, 0, 256), (5, 256, 512), (6, 0, 256), (6, 256, 512), (7, 0, 256), (7, 256, 384), (7, 384, 512)):
-            for g in (0, 1):
-                MM(i, 2, g, 0, lo, hi); MM(i, 2, g, 1, lo, hi)
-            R(i, 2, "S", lo, hi); SQ(i, 2, "V", lo, hi); ST(i, 1024 + lo, 1024 + hi)
+            subtract(i, 0)
+        quantise_w(0, 1, count=2)
+        expand(0, 1)
+        expand(1, 1)
+        quantise_rest(0, 0, count=2)
+        subtract(3, 0)
+        quantise_w(2, 1, count=2)
+        expand(2, 1)
+        expand(3, 1)
+
+        round_x(scalar, 0, 0, 0, count=2)
+        round_x(scalar, 0, 2, 0)
+        round_x(vector, 0, 3, 0)
+        quantise_rest(2, 0, count=2)
+        quantise_x(0, 0, 0)
+        subtract(0, 1)
+        quantise_x(0, 1, 0)
+        for tier in range(TIERS):
+            products(left, (0,), 0, tier)
+
+        round_x(scalar, 0, 0, 1, count=2)
+        round_x(scalar, 0, 2, 1)
+        subtract(1, 1)
+        round_x(vector, 0, 3, 1)
+        quantise_x(0, 0, 1)
+        quantise_rest(0, 1, count=2)
+        quantise_x(0, 1, 1)
+        subtract(2, 1)
+        products(left, (0,), 1, 0)
+        products((0, 1), (0,), 1, 1)
+
+        round_x(scalar, 1, 0, 0, count=2)
+        round_x(scalar, 1, 2, 0)
+        subtract(3, 1)
+        round_x(vector, 1, 3, 0)
+        quantise_rest(2, 1, count=2)
+        quantise_x(1, 0, 0)
+        quantise_x(1, 1, 0)
+        products((2, 3), (0,), 1, 1)
+        for i in left:
+            both_tiers(i, 1, 0)
+
+        relu(scalar, 0, 0)
+        round_x(scalar, 1, 3, 1)
+        round_x(vector, 1, 0, 1, count=2)
+        round_x(vector, 1, 2, 1)
+        quantise_x(1, 0, 1)
+        quantise_x(1, 1, 1)
+        relu(scalar, 1, 0)
+        relu(vector, 2, 0)
+        square(scalar, 0, 0, CHUNK)
+        relu(scalar, 3, 0)
+
+        round_w(vector, 4, 0)
+        round_w(scalar, 5, 0)
+        round_w(vector, 6, 0)
+        quantise_w(4, 0)
+        round_w(vector, 7, 0)
+        quantise_w(5, 0)
+        quantise_w(6, 0)
+        square(vector, 1, 0, CHUNK)
+        for i in (0, 1, 2):
+            both_tiers(i, 1, 1)
+        expand(4, 0)
+        both_tiers(3, 1, 1)
+        expand(5, 0)
+        for i in left:
+            relu(scalar, i, 1)
+
+        early = (0, 1)
+        subtract(4, 0)
+        subtract(5, 0)
+        products((4, 5), early, 0, 0)
+        expand(6, 0)
+        products((6,), early, 0, 0)
+        round_w(scalar, 5, 1)
+        round_w(scalar, 6, 1, count=2)
+        round_w(vector, 4, 1)
+        quantise_rest(4, 0)
+        quantise_rest(5, 0)
+        quantise_w(4, 1)
+        subtract(6, 0)
+        products((4,), early, 0, 1)
+        expand(4, 1)
+        products((5,), early, 0, 1)
+        quantise_w(5, 1)
+        quantise_w(6, 1)
+        quantise_rest(6, 0)
+        subtract(4, 1)
+        expand(5, 1)
+        products((4,), early, 1, 0)
+        products((6,), early, 0, 1)
+        for i in (0, 1):
+            square(scalar, i, CHUNK, 2 * CHUNK)
+            store(i, 0, 2 * CHUNK)
+        round_x(scalar, 2, 0, 0)
+        subtract(5, 1)
+        expand(6, 1)
+        products((5, 6), early, 1, 0)
+        quantise_rest(4, 1)
+        round_x(vector, 2, 2, 0)
+        quantise_rest(5, 1)
+        subtract(6, 1)
+        round_x(vector, 2, 3, 0)
+        quantise_rest(6, 1)
+        quantise_w(7, 0)
+        quantise_w(7, 1)
+        square(scalar, 2, 0, 2 * CHUNK)
+        store(2, 0, 2 * CHUNK)
+        round_x(scalar, 2, 1, 0)
+        square(scalar, 3, 0, 2 * CHUNK)
+        store(3, 0, 2 * CHUNK)
+        products((4, 5, 6), early, 1, 1)
+        expand(7, 0)
+        expand(7, 1)
+
+        quantise_x(2, 0, 0)
+        quantise_x(2, 1, 0)
+        round_x(vector, 2, 0, 1, count=2)
+        round_x(vector, 2, 2, 1, count=2)
+        quantise_x(2, 0, 1)
+        quantise_x(2, 1, 1)
+        relu(scalar, 4, 0)
+        relu(scalar, 4, 1)
+        relu(scalar, 5, 0)
+        for tier in range(TIERS):
+            products((0, 1, 2), (2,), 0, tier)
+        square(scalar, 4, 0, 2 * CHUNK)
+        store(4, 0, 2 * CHUNK)
+        relu(scalar, 5, 1)
+        relu(vector, 6, 0)
+        square(scalar, 5, 0, 2 * CHUNK)
+        store(5, 0, 2 * CHUNK)
+        relu(vector, 6, 1)
+        subtract(7, 0)
+        subtract(7, 1)
+        for i in (0, 1, 2):
+            both_tiers(i, 2, 1)
+        square(scalar, 6, 0, 2 * CHUNK)
+        store(6, 0, 2 * CHUNK)
+        quantise_rest(7, 0)
+        quantise_rest(7, 1)
+        for i in (0, 1, 2):
+            finish(i, 2)
+
+        pieces = [(i, t, 0, CHUNK) for i, t in ((3, 2), (4, 2), (7, 0), (7, 1))]
+        pieces.extend((i, 2, lo, lo + UNIT) for i in (5, 6) for lo in (0, UNIT))
+        pieces.extend([(7, 2, 0, UNIT), (7, 2, UNIT, UNIT + P), (7, 2, UNIT + P, CHUNK)])
+        for i, t, lo, hi in pieces:
+            for g in range(PASSES):
+                both_tiers(i, t, g, lo, hi)
+            finish(i, t, lo, hi)

@@ -18,26 +18,32 @@ PACK = 4
 K_PASS = P * PACK
 PASSES = K // K_PASS
 TIERS = 2
+BANDS = N // P
 CHUNK = 512
-UNIT = 256
+HALF = CHUNK // 2
 RUN = 4
 BANKS = 8
-ROUNDED_BUFS = 8
-REST_BUFS = 4
+LEFT = 5
 
 
 def tile_mix_tierw_relu2_kernel(tc, w, x, out):
     nc = tc.nc
     with ExitStack() as ctx:
         keep = ctx.enter_context(tc.tile_pool(name="keep", bufs=1))
-        stage = ctx.enter_context(tc.tile_pool(name="stage", bufs=ROUNDED_BUFS))
         psum = ctx.enter_context(tc.psum_pool(name="psum", bufs=1))
         ctx.enter_context(tc.manual_schedule())
 
         free_banks = list(range(BANKS))
         bank_of = {}
-        raw, rounded, rest, codes, scales = {}, {}, {}, {}, {}
-        expanded, sums, passes_done, result = {}, {}, {}, {}
+        raw, expanded, sums, columns_left, result = {}, {}, {}, {}, {}
+
+        grouped, codes, scales = {}, {}, {}
+        for g in range(PASSES):
+            for name, width in (("w", N), ("x", T)):
+                grouped[name, g] = keep.tile([P, PACK * width], BF16, name="grouped_%s%d" % (name, g), align_bytes=64)
+            for name, width in (("w_q", N), ("w_r", N), ("x", T)):
+                codes[name, g] = keep.tile([P, width], U32, name="codes_%s%d" % (name, g), align_bytes=256)
+                scales[name, g] = keep.tile([P, width], U8, name="scales_%s%d" % (name, g), align_bytes=256)
 
         def rows_view(ap):
             return ap.rearrange("p j (c i) -> p c j i", i=RUN)
@@ -45,120 +51,115 @@ def tile_mix_tierw_relu2_kernel(tc, w, x, out):
         def words_view(ap):
             return ap.rearrange("p (c i j) -> p c j i", i=RUN, j=PACK)
 
-        def load(name, panel, g):
+        def load(name, lo, hi, g):
             src = w if name == "w" else x
-            tile = keep.tile([P, PACK, CHUNK], F32, name="raw_%s_%d_%d" % (name, 2 * panel, g))
-            rows = src[g * K_PASS : (g + 1) * K_PASS, panel * CHUNK : (panel + 1) * CHUNK]
+            tile = keep.tile([P, PACK, hi - lo], F32, name="raw_%s_%d_%d" % (name, lo, g))
+            rows = src[g * K_PASS : (g + 1) * K_PASS, lo:hi]
             nc.sync.dma_start(out=tile[:], in_=rows.rearrange("(p j) n -> p j n", j=PACK))
-            for half in range(2):
-                raw[name, 2 * panel + half, g] = tile[:, :, half * UNIT : (half + 1) * UNIT]
+            for c in range(lo, hi, P):
+                raw[name, c, g] = (tile, lo)
 
-        def place(first, count):
-            lo = (first % 2) * P
-            return first // 2, lo, lo + count * P
+        def raw_columns(name, lo, hi, g):
+            tile, first = raw[name, lo, g]
+            return tile[:, :, lo - first : hi - first]
 
-        def round_columns(engine, key, lo, hi):
-            if key not in rounded:
-                rounded[key] = stage.tile([P, PACK * UNIT], BF16, name="grouped", align_bytes=64)
-            dst = words_view(rounded[key][:, PACK * lo : PACK * hi])
-            src = rows_view(raw[key][:, :, lo:hi])
+        def round_columns(engine, name, lo, hi, g):
+            dst = words_view(grouped[name, g][:, PACK * lo : PACK * hi])
+            src = rows_view(raw_columns(name, lo, hi, g))
             if engine is vector:
                 nc.vector.tensor_copy(out=dst, in_=src)
             else:
                 nc.scalar.copy(out=dst, in_=src)
 
         def round_w(engine, i, g, count=1):
-            unit, lo, hi = place(i, count)
-            round_columns(engine, ("w", unit, g), lo, hi)
+            round_columns(engine, "w", i * P, (i + count) * P, g)
 
         def round_x(engine, t, q, g, count=1):
-            unit, lo, hi = place(4 * t + q, count)
-            round_columns(engine, ("x", unit, g), lo, hi)
+            round_columns(engine, "x", t * CHUNK + q * P, t * CHUNK + (q + count) * P, g)
 
-        def quantise(key, width, lo, hi, values):
-            if key not in codes:
-                codes[key] = keep.tile([P, width], U32, name="codes_%s_%d_%d" % key, align_bytes=256)
-                scales[key] = keep.tile([P, width], U8, name="scales_%s_%d_%d" % key, align_bytes=256)
-            nc.vector.quantize_mx(out=codes[key][:, lo:hi].bitcast(FP8X4), scales=scales[key][:, lo:hi], in_=values)
+        def quantise(name, lo, hi, g):
+            nc.vector.quantize_mx(
+                out=codes[name, g][:, lo:hi].bitcast(FP8X4),
+                scales=scales[name, g][:, lo:hi],
+                in_=grouped[name[0], g][:, PACK * lo : PACK * hi],
+            )
 
         def quantise_w(i, g, count=1):
-            unit, lo, hi = place(i, count)
-            quantise(("w", unit, g), UNIT, lo, hi, rounded["w", unit, g][:, PACK * lo : PACK * hi])
+            quantise("w_q", i * P, (i + count) * P, g)
 
         def quantise_rest(i, g, count=1):
-            unit, lo, hi = place(i, count)
-            quantise(("r", unit, g), UNIT, lo, hi, rest[unit, g][:, PACK * lo : PACK * hi])
+            quantise("w_r", i * P, (i + count) * P, g)
 
         def quantise_x(t, half, g):
-            quantise(("x", t, g), CHUNK, half * UNIT, (half + 1) * UNIT, rounded["x", 2 * t + half, g][:])
+            quantise("x", t * CHUNK + half * HALF, t * CHUNK + (half + 1) * HALF, g)
 
         def take_bank(key, shape):
             bank_of[key] = free_banks.pop(0)
             return psum.tile(shape, F32, name="bank_%d" % bank_of[key])
 
         def expand(i, g):
-            unit, lo, hi = place(i, 1)
             expanded[i, g] = take_bank(("expanded", i, g), [P, PACK, P])
             for j in range(PACK):
                 nc.tensor.matmul_mx(
                     out=expanded[i, g][:, j, :],
                     lhsT=id_codes[:, j * P : (j + 1) * P].bitcast(FP8X4),
                     lhsT_scale=id_scales[:, j * P : (j + 1) * P],
-                    rhs=codes["w", unit, g][:, lo:hi].bitcast(FP8X4),
-                    rhs_scale=scales["w", unit, g][:, lo:hi],
+                    rhs=codes["w_q", g][:, i * P : (i + 1) * P].bitcast(FP8X4),
+                    rhs_scale=scales["w_q", g][:, i * P : (i + 1) * P],
                     start=True,
                     stop=True,
                 )
 
         def subtract(i, g):
-            unit, lo, hi = place(i, 1)
-            if (unit, g) not in rest:
-                rest[unit, g] = stage.tile([P, PACK * UNIT], BF16, name="resid", bufs=REST_BUFS, align_bytes=64)
             nc.vector.tensor_tensor(
-                out=words_view(rest[unit, g][:, PACK * lo : PACK * hi]),
-                in0=rows_view(raw["w", unit, g][:, :, lo:hi]),
+                out=words_view(grouped["w", g][:, PACK * i * P : PACK * (i + 1) * P]),
+                in0=rows_view(raw_columns("w", i * P, (i + 1) * P, g)),
                 in1=rows_view(expanded[i, g][:]),
                 op=ALU.subtract,
             )
             free_banks.append(bank_of["expanded", i, g])
 
-        def product(i, t, g, tier, lo=0, hi=CHUNK):
-            key = ("sum", i, t, lo)
-            if key not in sums:
-                sums[key] = take_bank(key, [P, hi - lo])
-                passes_done[key] = 0
-            passes_done[key] = passes_done[key] + 1
-            unit, w_lo, w_hi = place(i, 1)
-            operand = ("wr"[tier], unit, g)
+        def product(i, g, tier, lo, hi, first, width):
+            key = (i, first)
+            start = key not in sums
+            if start:
+                sums[key] = take_bank(key, [P, width])
+                columns_left[key] = TIERS * PASSES * width
+            columns_left[key] = columns_left[key] - (hi - lo)
+            operand = (("w_q", "w_r")[tier], g)
             nc.tensor.matmul_mx(
-                out=sums[key][:],
-                lhsT=codes[operand][:, w_lo:w_hi].bitcast(FP8X4),
-                lhsT_scale=scales[operand][:, w_lo:w_hi],
-                rhs=codes["x", t, g][:, lo:hi].bitcast(FP8X4),
-                rhs_scale=scales["x", t, g][:, lo:hi],
-                start=passes_done[key] == 1,
-                stop=passes_done[key] == TIERS * PASSES,
+                out=sums[key][:, lo - first : hi - first],
+                lhsT=codes[operand][:, i * P : (i + 1) * P].bitcast(FP8X4),
+                lhsT_scale=scales[operand][:, i * P : (i + 1) * P],
+                rhs=codes["x", g][:, lo:hi].bitcast(FP8X4),
+                rhs_scale=scales["x", g][:, lo:hi],
+                start=start,
+                stop=columns_left[key] == 0,
             )
 
-        def products(bands, chunks, g, tier):
+        def products(bands, chunks, g, tiers):
             for i in bands:
                 for t in chunks:
-                    product(i, t, g, tier)
+                    for tier in tiers:
+                        product(i, g, tier, t * CHUNK, (t + 1) * CHUNK, t * CHUNK, CHUNK)
 
-        def both_tiers(i, t, g, lo=0, hi=CHUNK):
-            for tier in range(TIERS):
-                product(i, t, g, tier, lo, hi)
+        def half_products(bands, t, half, g, tiers):
+            lo = t * CHUNK + half * HALF
+            for i in bands:
+                for tier in tiers:
+                    product(i, g, tier, lo, lo + HALF, t * CHUNK, CHUNK)
 
-        def relu(engine, i, t, lo=0, hi=CHUNK):
+        def relu(engine, i, lo, hi):
             if i not in result:
                 result[i] = keep.tile([P, T], F32, name="res_%d" % i)
-            key = ("sum", i, t, lo)
-            dst = result[i][:, t * CHUNK + lo : t * CHUNK + hi]
             if engine is vector:
-                nc.vector.tensor_scalar_max(out=dst, in0=sums[key][:], scalar1=0.0)
+                nc.vector.tensor_scalar_max(out=result[i][:, lo:hi], in0=sums[i, lo][:], scalar1=0.0)
             else:
-                nc.scalar.activation(out=dst, in_=sums[key][:], func=ACT.Relu)
-            free_banks.append(bank_of[key])
+                nc.scalar.activation(out=result[i][:, lo:hi], in_=sums[i, lo][:], func=ACT.Relu)
+            free_banks.append(bank_of[i, lo])
+
+        def relu_chunk(engine, i, t):
+            relu(engine, i, t * CHUNK, (t + 1) * CHUNK)
 
         def square(engine, i, lo, hi):
             dst = result[i][:, lo:hi]
@@ -170,20 +171,24 @@ def tile_mix_tierw_relu2_kernel(tc, w, x, out):
         def store(i, lo, hi):
             nc.sync.dma_start(out=out[i * P : (i + 1) * P, lo:hi], in_=result[i][:, lo:hi])
 
-        def finish(i, t, lo=0, hi=CHUNK):
-            relu(scalar, i, t, lo, hi)
-            square(vector, i, t * CHUNK + lo, t * CHUNK + hi)
-            store(i, t * CHUNK + lo, t * CHUNK + hi)
+        def finish(i, lo, hi):
+            relu(scalar, i, lo, hi)
+            square(vector, i, lo, hi)
+            store(i, lo, hi)
 
         vector, scalar = nc.vector, nc.scalar
-        left = range(4)
+        left = range(LEFT)
+        right = range(LEFT, BANDS)
+        both = range(TIERS)
         identity = keep.tile([P, PACK * K_PASS], BF16, name="ident", align_bytes=64)
         id_codes = keep.tile([P, K_PASS], U32, name="id_codes", align_bytes=256)
         id_scales = keep.tile([P, K_PASS], U8, name="id_scales", align_bytes=256)
 
-        for name, panel in (("w", 0), ("x", 0), ("x", 1), ("w", 1), ("x", 2)):
+        for name, lo, hi in (
+            ("w", 0, LEFT * P), ("x", 0, CHUNK), ("x", CHUNK, 2 * CHUNK), ("w", LEFT * P, N), ("x", 2 * CHUNK, T)
+        ):
             for g in range(PASSES):
-                load(name, panel, g)
+                load(name, lo, hi, g)
 
         one_hot = keep.tile([P, K_PASS + PACK], BF16, name="ramp")
         nc.vector.memset(one_hot[:], 0.0)
@@ -200,163 +205,167 @@ def tile_mix_tierw_relu2_kernel(tc, w, x, out):
                 nc.vector.tensor_copy(out=dst, in_=src)
         nc.vector.quantize_mx(out=id_codes[:].bitcast(FP8X4), scales=id_scales[:], in_=identity[:])
 
-        for i in left:
-            round_w(scalar if i % 2 else vector, i, 0)
-        for i in left:
+        round_w(vector, 0, 0)
+        round_w(scalar, 3, 0)
+        round_w(vector, 1, 0)
+        quantise_w(0, 0)
+        expand(0, 0)
+        round_w(vector, 2, 0)
+        round_w(scalar, 4, 0)
+        for i in (1, 3, 2, 4):
             quantise_w(i, 0)
             expand(i, 0)
-        round_w(scalar, 0, 1, count=2)
-        round_w(scalar, 2, 1, count=2)
-        for i in (0, 1, 2):
+        for i in range(4):
+            round_w(scalar, i, 1)
+        for i in (0, 1, 3):
             subtract(i, 0)
-        quantise_w(0, 1, count=2)
+        quantise_w(0, 1)
         expand(0, 1)
+        subtract(2, 0)
+        quantise_w(1, 1)
         expand(1, 1)
-        quantise_rest(0, 0, count=2)
-        subtract(3, 0)
-        quantise_w(2, 1, count=2)
+        subtract(4, 0)
+        quantise_w(2, 1)
         expand(2, 1)
+        round_x(scalar, 0, 0, 0)
+        round_x(vector, 0, 1, 0)
+        quantise_rest(0, 0, count=2)
+        round_x(scalar, 0, 2, 0, count=2)
+        round_w(scalar, 4, 1)
+        quantise_w(3, 1)
         expand(3, 1)
-
-        round_x(scalar, 0, 0, 0, count=2)
-        round_x(scalar, 0, 2, 0)
-        round_x(vector, 0, 3, 0)
-        quantise_rest(2, 0, count=2)
         quantise_x(0, 0, 0)
+        quantise_rest(2, 0, count=2)
+        half_products((0, 1, 2, 3), 0, 0, 0, both)
         subtract(0, 1)
+        quantise_rest(4, 0)
+        half_products((4,), 0, 0, 0, both)
         quantise_x(0, 1, 0)
-        for tier in range(TIERS):
-            products(left, (0,), 0, tier)
+        subtract(1, 1)
+        quantise_w(4, 1)
+        half_products(left, 0, 1, 0, both)
+        expand(4, 1)
 
         round_x(scalar, 0, 0, 1, count=2)
-        round_x(scalar, 0, 2, 1)
-        subtract(1, 1)
-        round_x(vector, 0, 3, 1)
-        quantise_x(0, 0, 1)
-        quantise_rest(0, 1, count=2)
-        quantise_x(0, 1, 1)
+        round_x(scalar, 0, 2, 1, count=2)
         subtract(2, 1)
-        products(left, (0,), 1, 0)
-        products((0, 1), (0,), 1, 1)
+        quantise_rest(0, 1, count=2)
+        quantise_x(0, 0, 1)
+        subtract(3, 1)
+        quantise_rest(2, 1)
+        half_products(left, 0, 0, 1, (0,))
+        half_products((0, 1, 2), 0, 0, 1, (1,))
+        quantise_x(0, 1, 1)
+        subtract(4, 1)
+        quantise_rest(3, 1)
+        quantise_rest(4, 1)
+        half_products((0, 1, 2), 0, 1, 1, both)
+        half_products((3, 4), 0, 1, 1, (0,))
+        products((3, 4), (0,), 1, (1,))
 
         round_x(scalar, 1, 0, 0, count=2)
-        round_x(scalar, 1, 2, 0)
-        subtract(3, 1)
-        round_x(vector, 1, 3, 0)
-        quantise_rest(2, 1, count=2)
+        round_x(scalar, 1, 2, 0, count=2)
         quantise_x(1, 0, 0)
+        relu_chunk(vector, 0, 0)
+        relu_chunk(scalar, 1, 0)
+        half_products(left, 1, 0, 0, both)
         quantise_x(1, 1, 0)
-        products((2, 3), (0,), 1, 1)
-        for i in left:
-            both_tiers(i, 1, 0)
-
-        relu(scalar, 0, 0)
-        round_x(scalar, 1, 3, 1)
+        half_products(left, 1, 1, 0, both)
         round_x(vector, 1, 0, 1, count=2)
+        round_x(scalar, 1, 3, 1)
         round_x(vector, 1, 2, 1)
         quantise_x(1, 0, 1)
         quantise_x(1, 1, 1)
-        relu(scalar, 1, 0)
-        relu(vector, 2, 0)
+        for i in (2, 3, 4):
+            relu_chunk(scalar, i, 0)
         square(scalar, 0, 0, CHUNK)
-        relu(scalar, 3, 0)
-
-        round_w(vector, 4, 0)
-        round_w(scalar, 5, 0)
+        products((0, 1), (1,), 1, both)
+        round_w(vector, 5, 0)
         round_w(vector, 6, 0)
-        quantise_w(4, 0)
-        round_w(vector, 7, 0)
         quantise_w(5, 0)
+        round_w(vector, 7, 0)
         quantise_w(6, 0)
-        square(vector, 1, 0, CHUNK)
-        for i in (0, 1, 2):
-            both_tiers(i, 1, 1)
-        expand(4, 0)
-        both_tiers(3, 1, 1)
         expand(5, 0)
-        for i in left:
-            relu(scalar, i, 1)
+        products((2,), (1,), 1, both)
+        expand(6, 0)
+        round_w(vector, 5, 1)
+        quantise_w(7, 0)
+        round_w(vector, 6, 1)
+        quantise_w(5, 1)
+        products((3,), (1,), 1, both)
+        expand(5, 1)
+        subtract(5, 0)
+        quantise_w(6, 1)
+        products((4,), (1,), 1, both)
+        expand(6, 1)
+        relu_chunk(scalar, 0, 1)
+        relu_chunk(scalar, 1, 1)
+        square(scalar, 0, CHUNK, 2 * CHUNK)
+        store(0, 0, 2 * CHUNK)
+        relu_chunk(scalar, 2, 1)
 
         early = (0, 1)
-        subtract(4, 0)
-        subtract(5, 0)
-        products((4, 5), early, 0, 0)
-        expand(6, 0)
-        products((6,), early, 0, 0)
-        round_w(scalar, 5, 1)
-        round_w(scalar, 6, 1, count=2)
-        round_w(vector, 4, 1)
-        quantise_rest(4, 0)
-        quantise_rest(5, 0)
-        quantise_w(4, 1)
         subtract(6, 0)
-        products((4,), early, 0, 1)
-        expand(4, 1)
-        products((5,), early, 0, 1)
-        quantise_w(5, 1)
-        quantise_w(6, 1)
-        quantise_rest(6, 0)
-        subtract(4, 1)
-        expand(5, 1)
-        products((4,), early, 1, 0)
-        products((6,), early, 0, 1)
-        for i in (0, 1):
-            square(scalar, i, CHUNK, 2 * CHUNK)
-            store(i, 0, 2 * CHUNK)
-        round_x(scalar, 2, 0, 0)
+        quantise_rest(5, 0)
+        round_w(vector, 7, 1)
         subtract(5, 1)
-        expand(6, 1)
-        products((5, 6), early, 1, 0)
-        quantise_rest(4, 1)
-        round_x(vector, 2, 2, 0)
-        quantise_rest(5, 1)
-        subtract(6, 1)
-        round_x(vector, 2, 3, 0)
-        quantise_rest(6, 1)
-        quantise_w(7, 0)
+        quantise_rest(6, 0)
         quantise_w(7, 1)
-        square(scalar, 2, 0, 2 * CHUNK)
-        store(2, 0, 2 * CHUNK)
-        round_x(scalar, 2, 1, 0)
-        square(scalar, 3, 0, 2 * CHUNK)
-        store(3, 0, 2 * CHUNK)
-        products((4, 5, 6), early, 1, 1)
+        for g in range(PASSES):
+            products((5,), early, g, (0,))
         expand(7, 0)
+        relu_chunk(scalar, 3, 1)
+        square(scalar, 1, 0, 2 * CHUNK)
+        store(1, 0, 2 * CHUNK)
+        relu_chunk(scalar, 4, 1)
+        subtract(6, 1)
+        quantise_rest(5, 1)
+        products((5,), early, 0, (1,))
         expand(7, 1)
-
+        products((5,), early, 1, (1,))
+        round_x(vector, 2, 0, 0, count=2)
+        quantise_rest(6, 1)
+        subtract(7, 0)
+        round_x(vector, 2, 2, 0, count=2)
+        quantise_rest(7, 0)
+        subtract(7, 1)
         quantise_x(2, 0, 0)
+        quantise_rest(7, 1)
         quantise_x(2, 1, 0)
+        for i in (6, 7):
+            for g in range(PASSES):
+                products((i,), early, g, both)
         round_x(vector, 2, 0, 1, count=2)
         round_x(vector, 2, 2, 1, count=2)
+        for i in (2, 3, 4):
+            square(scalar, i, 0, 2 * CHUNK)
+            store(i, 0, 2 * CHUNK)
         quantise_x(2, 0, 1)
         quantise_x(2, 1, 1)
-        relu(scalar, 4, 0)
-        relu(scalar, 4, 1)
-        relu(scalar, 5, 0)
-        for tier in range(TIERS):
-            products((0, 1, 2), (2,), 0, tier)
-        square(scalar, 4, 0, 2 * CHUNK)
-        store(4, 0, 2 * CHUNK)
-        relu(scalar, 5, 1)
-        relu(vector, 6, 0)
+
+        for t in early:
+            relu_chunk(scalar, 5, t)
+        relu_chunk(scalar, 6, 0)
         square(scalar, 5, 0, 2 * CHUNK)
         store(5, 0, 2 * CHUNK)
-        relu(vector, 6, 1)
-        subtract(7, 0)
-        subtract(7, 1)
-        for i in (0, 1, 2):
-            both_tiers(i, 2, 1)
-        square(scalar, 6, 0, 2 * CHUNK)
+        relu_chunk(vector, 6, 1)
+        relu_chunk(vector, 7, 0)
+        square(vector, 6, 0, 2 * CHUNK)
         store(6, 0, 2 * CHUNK)
-        quantise_rest(7, 0)
-        quantise_rest(7, 1)
-        for i in (0, 1, 2):
-            finish(i, 2)
-
-        pieces = [(i, t, 0, CHUNK) for i, t in ((3, 2), (4, 2), (7, 0), (7, 1))]
-        pieces.extend((i, 2, lo, lo + UNIT) for i in (5, 6) for lo in (0, UNIT))
-        pieces.extend([(7, 2, 0, UNIT), (7, 2, UNIT, UNIT + P), (7, 2, UNIT + P, CHUNK)])
-        for i, t, lo, hi in pieces:
+        relu_chunk(scalar, 7, 1)
+        square(scalar, 7, 0, CHUNK)
+        square(vector, 7, CHUNK, 2 * CHUNK)
+        store(7, 0, 2 * CHUNK)
+        last = 2 * CHUNK
+        for g in range(PASSES):
+            products((0, 1), (2,), g, both)
+        for i in (0, 1):
+            finish(i, last, T)
+        pieces = [(i, last, T) for i in (2, 3, 4)]
+        pieces.extend((i, lo, lo + HALF) for i in (5, 6) for lo in (last, last + HALF))
+        pieces.extend([(7, last, last + HALF), (7, last + HALF, T - P), (7, T - P, T)])
+        for i, lo, hi in pieces:
             for g in range(PASSES):
-                both_tiers(i, t, g, lo, hi)
-            finish(i, t, lo, hi)
+                for tier in both:
+                    product(i, g, tier, lo, hi, lo, hi - lo)
+            finish(i, lo, hi)

@@ -53,7 +53,7 @@ def tile_mix_tierw_relu2_kernel(tc, w, x, out):
 
         def load(name, lo, hi, g):
             src = w if name == "w" else x
-            tile = keep.tile([P, PACK, hi - lo], F32, name="raw_%s_%d_%d" % (name, lo, g))
+            tile = keep.tile([P, PACK, hi - lo], F32, name="raw_%s_%d_%d" % (name, lo, g), align_bytes=256)
             rows = src[g * K_PASS : (g + 1) * K_PASS, lo:hi]
             nc.sync.dma_start(out=tile[:], in_=rows.rearrange("(p j) n -> p j n", j=PACK))
             for c in range(lo, hi, P):
@@ -151,7 +151,7 @@ def tile_mix_tierw_relu2_kernel(tc, w, x, out):
 
         def relu(engine, i, lo, hi):
             if i not in result:
-                result[i] = keep.tile([P, T], F32, name="res_%d" % i)
+                result[i] = keep.tile([P, T], F32, name="res_%d" % i, align_bytes=256)
             if engine is vector:
                 nc.vector.tensor_scalar_max(out=result[i][:, lo:hi], in0=sums[i, lo][:], scalar1=0.0)
             else:

@@ -19,11 +19,9 @@ K_PASS = P * PACK
 PASSES = K // K_PASS
 TIERS = 2
 BANDS = N // P
-CHUNK = 512
-HALF = CHUNK // 2
+CHUNK = 4
 RUN = 4
-BANKS = 8
-LEFT = 5
+SCALAR_PART = 3
 
 
 def tile_mix_tierw_relu2_kernel(tc, w, x, out):
@@ -33,17 +31,19 @@ def tile_mix_tierw_relu2_kernel(tc, w, x, out):
         psum = ctx.enter_context(tc.psum_pool(name="psum", bufs=1))
         ctx.enter_context(tc.manual_schedule())
 
-        free_banks = list(range(BANKS))
-        bank_of = {}
         raw, expanded, sums, columns_left, result = {}, {}, {}, {}, {}
-
         grouped, codes, scales = {}, {}, {}
         for g in range(PASSES):
             for name, width in (("w", N), ("x", T)):
-                grouped[name, g] = keep.tile([P, PACK * width], BF16, name="grouped_%s%d" % (name, g), align_bytes=64)
+                grouped[name, g] = keep.tile([P, PACK * width], BF16, name="grouped_%s%d" % (name, g), align_bytes=256)
             for name, width in (("w_q", N), ("w_r", N), ("x", T)):
                 codes[name, g] = keep.tile([P, width], U32, name="codes_%s%d" % (name, g), align_bytes=256)
                 scales[name, g] = keep.tile([P, width], U8, name="scales_%s%d" % (name, g), align_bytes=256)
+        for i in range(BANDS):
+            result[i] = keep.tile([P, T], F32, name="res_%d" % i, align_bytes=256)
+        identity = keep.tile([P, PACK * K_PASS], BF16, name="ident", align_bytes=256)
+        id_codes = keep.tile([P, K_PASS], U32, name="id_codes", align_bytes=256)
+        id_scales = keep.tile([P, K_PASS], U8, name="id_scales", align_bytes=256)
 
         def rows_view(ap):
             return ap.rearrange("p j (c i) -> p c j i", i=RUN)
@@ -51,321 +51,197 @@ def tile_mix_tierw_relu2_kernel(tc, w, x, out):
         def words_view(ap):
             return ap.rearrange("p (c i j) -> p c j i", i=RUN, j=PACK)
 
-        def load(name, lo, hi, g):
+        def load(name, g, lo, hi):
             src = w if name == "w" else x
-            tile = keep.tile([P, PACK, hi - lo], F32, name="raw_%s_%d_%d" % (name, lo, g), align_bytes=256)
-            rows = src[g * K_PASS : (g + 1) * K_PASS, lo:hi]
+            tile = keep.tile([P, PACK, (hi - lo) * P], F32, name="raw_%s_%d_%d" % (name, lo, g), align_bytes=256)
+            rows = src[g * K_PASS : (g + 1) * K_PASS, lo * P : hi * P]
             nc.sync.dma_start(out=tile[:], in_=rows.rearrange("(p j) n -> p j n", j=PACK))
-            for c in range(lo, hi, P):
-                raw[name, c, g] = (tile, lo)
+            for s in range(lo, hi):
+                raw[name, g, s] = (tile, lo)
 
-        def raw_columns(name, lo, hi, g):
-            tile, first = raw[name, lo, g]
-            return tile[:, :, lo - first : hi - first]
+        def raw_columns(name, g, lo, hi):
+            tile, first = raw[name, g, lo]
+            return tile[:, :, (lo - first) * P : (hi - first) * P]
 
-        def round_columns(engine, name, lo, hi, g):
-            dst = words_view(grouped[name, g][:, PACK * lo : PACK * hi])
-            src = rows_view(raw_columns(name, lo, hi, g))
-            if engine is vector:
-                nc.vector.tensor_copy(out=dst, in_=src)
-            else:
-                nc.scalar.copy(out=dst, in_=src)
+        def rnd(engine, name, g, lo, hi):
+            def call():
+                dst = words_view(grouped[name, g][:, K_PASS * lo : K_PASS * hi])
+                src = rows_view(raw_columns(name, g, lo, hi))
+                if engine is nc.vector:
+                    nc.vector.tensor_copy(out=dst, in_=src)
+                elif engine is nc.scalar:
+                    nc.scalar.copy(out=dst, in_=src)
+                else:
+                    nc.gpsimd.tensor_scalar(out=dst, in0=src, scalar1=1.0, scalar2=0.0, op0=ALU.mult, op1=ALU.add)
+            return (call, [], [("rounded", name, g, s) for s in range(lo, hi)])
 
-        def round_w(engine, i, g, count=1):
-            round_columns(engine, "w", i * P, (i + count) * P, g)
-
-        def round_x(engine, t, q, g, count=1):
-            round_columns(engine, "x", t * CHUNK + q * P, t * CHUNK + (q + count) * P, g)
-
-        def quantise(name, lo, hi, g):
-            nc.vector.quantize_mx(
-                out=codes[name, g][:, lo:hi].bitcast(FP8X4),
-                scales=scales[name, g][:, lo:hi],
-                in_=grouped[name[0], g][:, PACK * lo : PACK * hi],
-            )
-
-        def quantise_w(i, g, count=1):
-            quantise("w_q", i * P, (i + count) * P, g)
-
-        def quantise_rest(i, g, count=1):
-            quantise("w_r", i * P, (i + count) * P, g)
-
-        def quantise_x(t, half, g):
-            quantise("x", t * CHUNK + half * HALF, t * CHUNK + (half + 1) * HALF, g)
-
-        def take_bank(key, shape):
-            bank_of[key] = free_banks.pop(0)
-            return psum.tile(shape, F32, name="bank_%d" % bank_of[key])
-
-        def expand(i, g):
-            expanded[i, g] = take_bank(("expanded", i, g), [P, PACK, P])
-            for j in range(PACK):
-                nc.tensor.matmul_mx(
-                    out=expanded[i, g][:, j, :],
-                    lhsT=id_codes[:, j * P : (j + 1) * P].bitcast(FP8X4),
-                    lhsT_scale=id_scales[:, j * P : (j + 1) * P],
-                    rhs=codes["w_q", g][:, i * P : (i + 1) * P].bitcast(FP8X4),
-                    rhs_scale=scales["w_q", g][:, i * P : (i + 1) * P],
-                    start=True,
-                    stop=True,
+        def quant(name, g, lo, hi):
+            def call():
+                nc.vector.quantize_mx(
+                    out=codes[name, g][:, lo * P : hi * P].bitcast(FP8X4),
+                    scales=scales[name, g][:, lo * P : hi * P],
+                    in_=grouped[name[0], g][:, K_PASS * lo : K_PASS * hi],
                 )
+            source = {"w_q": "w", "w_r": "rest", "x": "x"}[name]
+            return (call, [("rounded", source, g, s) for s in range(lo, hi)], [(name, g, s) for s in range(lo, hi)])
 
-        def subtract(i, g):
-            nc.vector.tensor_tensor(
-                out=words_view(grouped["w", g][:, PACK * i * P : PACK * (i + 1) * P]),
-                in0=rows_view(raw_columns("w", i * P, (i + 1) * P, g)),
-                in1=rows_view(expanded[i, g][:]),
-                op=ALU.subtract,
-            )
-            free_banks.append(bank_of["expanded", i, g])
+        busy = set()
 
-        def product(i, g, tier, lo, hi, first, width):
+        def expand(i, g, bank):
+            def call():
+                expanded[i, g] = (psum.tile([P, PACK, P], F32, name="bank_%d" % bank), bank)
+                busy.add(bank)
+                for j in range(PACK):
+                    nc.tensor.matmul_mx(
+                        out=expanded[i, g][0][:, j, :],
+                        lhsT=id_codes[:, j * P : (j + 1) * P].bitcast(FP8X4),
+                        lhsT_scale=id_scales[:, j * P : (j + 1) * P],
+                        rhs=codes["w_q", g][:, i * P : (i + 1) * P].bitcast(FP8X4),
+                        rhs_scale=scales["w_q", g][:, i * P : (i + 1) * P],
+                        start=True,
+                        stop=True,
+                    )
+            return (call, [("w_q", g, i), ("bank", bank)] + [("identity", j) for j in range(PACK)], [("expanded", g, i)])
+
+        def sub(i, g):
+            def call():
+                tile, bank = expanded[i, g]
+                nc.vector.tensor_tensor(
+                    out=words_view(grouped["w", g][:, K_PASS * i : K_PASS * (i + 1)]),
+                    in0=rows_view(raw_columns("w", g, i, i + 1)),
+                    in1=rows_view(tile[:]),
+                    op=ALU.subtract,
+                )
+                busy.remove(bank)
+            return (call, [("expanded", g, i)], [("rounded", "rest", g, i)])
+
+        home = {}
+
+        def place(i, lo, hi, bank):
+            for s in range(lo, hi):
+                home[i, s] = (lo, hi, bank)
+
+        opened = set()
+
+        def mm(i, g, tier, lo, hi):
+            first, end, bank = home[i, lo]
             key = (i, first)
-            start = key not in sums
-            if start:
-                sums[key] = take_bank(key, [P, width])
-                columns_left[key] = TIERS * PASSES * width
-            columns_left[key] = columns_left[key] - (hi - lo)
+            start = key not in opened
+            opened.add(key)
+            columns_left[key] = columns_left.get(key, TIERS * PASSES * (end - first)) - (hi - lo)
+            stop = columns_left[key] == 0
             operand = (("w_q", "w_r")[tier], g)
-            nc.tensor.matmul_mx(
-                out=sums[key][:, lo - first : hi - first],
-                lhsT=codes[operand][:, i * P : (i + 1) * P].bitcast(FP8X4),
-                lhsT_scale=scales[operand][:, i * P : (i + 1) * P],
-                rhs=codes["x", g][:, lo:hi].bitcast(FP8X4),
-                rhs_scale=scales["x", g][:, lo:hi],
-                start=start,
-                stop=columns_left[key] == 0,
-            )
 
-        def products(bands, chunks, g, tiers):
-            for i in bands:
-                for t in chunks:
-                    for tier in tiers:
-                        product(i, g, tier, t * CHUNK, (t + 1) * CHUNK, t * CHUNK, CHUNK)
+            def call():
+                if start:
+                    sums[key] = psum.tile([P, (end - first) * P], F32, name="bank_%d" % bank)
+                    busy.add(bank)
+                nc.tensor.matmul_mx(
+                    out=sums[key][:, (lo - first) * P : (hi - first) * P],
+                    lhsT=codes[operand][:, i * P : (i + 1) * P].bitcast(FP8X4),
+                    lhsT_scale=scales[operand][:, i * P : (i + 1) * P],
+                    rhs=codes["x", g][:, lo * P : hi * P].bitcast(FP8X4),
+                    rhs_scale=scales["x", g][:, lo * P : hi * P],
+                    start=start,
+                    stop=stop,
+                )
+            needs = [operand + (i,)] + [("x", g, s) for s in range(lo, hi)] + ([("bank", bank)] if start else [])
+            return (call, needs, [("summed", i, first)] if stop else [])
 
-        def half_products(bands, t, half, g, tiers):
-            lo = t * CHUNK + half * HALF
-            for i in bands:
-                for tier in tiers:
-                    product(i, g, tier, lo, lo + HALF, t * CHUNK, CHUNK)
+        def relu(engine, i, lo):
+            first, end, bank = home[i, lo]
 
-        def relu(engine, i, lo, hi):
-            if i not in result:
-                result[i] = keep.tile([P, T], F32, name="res_%d" % i, align_bytes=256)
-            if engine is vector:
-                nc.vector.tensor_scalar_max(out=result[i][:, lo:hi], in0=sums[i, lo][:], scalar1=0.0)
-            else:
-                nc.scalar.activation(out=result[i][:, lo:hi], in_=sums[i, lo][:], func=ACT.Relu)
-            free_banks.append(bank_of[i, lo])
-
-        def relu_chunk(engine, i, t):
-            relu(engine, i, t * CHUNK, (t + 1) * CHUNK)
+            def call():
+                dst = result[i][:, first * P : end * P]
+                if engine is nc.vector:
+                    nc.vector.tensor_scalar_max(out=dst, in0=sums[i, first][:], scalar1=0.0)
+                else:
+                    nc.scalar.activation(out=dst, in_=sums[i, first][:], func=ACT.Relu)
+                busy.remove(bank)
+            return (call, [("summed", i, first)], [("positive", i, s) for s in range(first, end)])
 
         def square(engine, i, lo, hi):
-            dst = result[i][:, lo:hi]
-            if engine is vector:
-                nc.vector.tensor_tensor(out=dst, in0=dst, in1=dst, op=ALU.mult)
-            else:
-                nc.scalar.activation(out=dst, in_=dst, func=ACT.Square)
+            def call():
+                dst = result[i][:, lo * P : hi * P]
+                if engine is nc.scalar:
+                    nc.scalar.activation(out=dst, in_=dst, func=ACT.Square)
+                else:
+                    engine.tensor_tensor(out=dst, in0=dst, in1=dst, op=ALU.mult)
+            return (call, [("positive", i, s) for s in range(lo, hi)], [("squared", i, s) for s in range(lo, hi)])
 
         def store(i, lo, hi):
-            nc.sync.dma_start(out=out[i * P : (i + 1) * P, lo:hi], in_=result[i][:, lo:hi])
+            def call():
+                nc.sync.dma_start(out=out[i * P : (i + 1) * P, lo * P : hi * P], in_=result[i][:, lo * P : hi * P])
+            return (call, [("squared", i, s) for s in range(lo, hi)], [])
 
-        def finish(i, lo, hi):
-            relu(scalar, i, lo, hi)
-            square(vector, i, lo, hi)
-            store(i, lo, hi)
+        def issue(queues):
+            facts = set()
+            at = [0] * len(queues)
+            while any(at[q] < len(queues[q]) for q in range(len(queues))):
+                moved = False
+                for q in range(len(queues)):
+                    while at[q] < len(queues[q]):
+                        call, needs, makes = queues[q][at[q]]
+                        if not all((f[1] not in busy) if f[0] == "bank" else (f in facts) for f in needs):
+                            break
+                        call()
+                        for f in makes:
+                            facts.add(f)
+                        at[q] = at[q] + 1
+                        moved = True
+                assert moved, at
 
-        vector, scalar = nc.vector, nc.scalar
-        left = range(LEFT)
-        right = range(LEFT, BANDS)
-        both = range(TIERS)
-        identity = keep.tile([P, PACK * K_PASS], BF16, name="ident", align_bytes=64)
-        id_codes = keep.tile([P, K_PASS], U32, name="id_codes", align_bytes=256)
-        id_scales = keep.tile([P, K_PASS], U8, name="id_scales", align_bytes=256)
+        V, S, G = nc.vector, nc.scalar, nc.gpsimd
+        both = (0, 1)
 
-        for name, lo, hi in (
-            ("w", 0, LEFT * P), ("x", 0, CHUNK), ("x", CHUNK, 2 * CHUNK), ("w", LEFT * P, N), ("x", 2 * CHUNK, T)
-        ):
-            for g in range(PASSES):
-                load(name, lo, hi, g)
+        def mms(bands, g, tiers, lo, hi):
+            return [mm(i, g, tier, lo, hi) for i in bands for tier in tiers]
 
-        one_hot = keep.tile([P, K_PASS + PACK], BF16, name="ramp")
-        nc.vector.memset(one_hot[:], 0.0)
-        nc.gpsimd.affine_select(
-            out=one_hot[:], in_=one_hot[:], compare_op=ALU.not_equal, fill=1.0,
-            base=PACK - 1, pattern=[[-1, K_PASS + PACK]], channel_multiplier=PACK,
-        )
-        for j in range(PACK):
-            dst = identity[:, j * K_PASS : (j + 1) * K_PASS]
-            src = one_hot[:, PACK - 1 - j : PACK - 1 - j + K_PASS]
-            if j == 0:
-                nc.scalar.activation(out=dst, in_=src, func=ACT.Square)
-            else:
-                nc.vector.tensor_copy(out=dst, in_=src)
-        nc.vector.quantize_mx(out=id_codes[:].bitcast(FP8X4), scales=id_scales[:], in_=identity[:])
+        def make_identity():
+            one_hot = keep.tile([P, K_PASS + PACK], BF16, name="ramp")
+            nc.gpsimd.memset(one_hot[:].bitcast(U32), 0)
+            nc.gpsimd.affine_select(
+                out=one_hot[:], in_=one_hot[:], compare_op=ALU.not_equal, fill=1.0,
+                base=PACK - 1, pattern=[[-1, K_PASS + PACK]], channel_multiplier=PACK,
+            )
+            for j in range(PACK):
+                dst = identity[:, j * K_PASS : (j + 1) * K_PASS]
+                src = one_hot[:, PACK - 1 - j : PACK - 1 - j + K_PASS]
+                if j == SCALAR_PART:
+                    nc.scalar.activation(out=dst, in_=src, func=ACT.Square)
+                else:
+                    nc.vector.tensor_copy(out=dst, in_=src)
 
-        round_w(vector, 0, 0)
-        round_w(scalar, 3, 0)
-        round_w(vector, 1, 0)
-        quantise_w(0, 0)
-        expand(0, 0)
-        round_w(vector, 2, 0)
-        round_w(scalar, 4, 0)
-        for i in (1, 3, 2, 4):
-            quantise_w(i, 0)
-            expand(i, 0)
-        for i in range(4):
-            round_w(scalar, i, 1)
-        for i in (0, 1, 3):
-            subtract(i, 0)
-        quantise_w(0, 1)
-        expand(0, 1)
-        subtract(2, 0)
-        quantise_w(1, 1)
-        expand(1, 1)
-        subtract(4, 0)
-        quantise_w(2, 1)
-        expand(2, 1)
-        round_x(scalar, 0, 0, 0)
-        round_x(vector, 0, 1, 0)
-        quantise_rest(0, 0, count=2)
-        round_x(scalar, 0, 2, 0, count=2)
-        round_w(scalar, 4, 1)
-        quantise_w(3, 1)
-        expand(3, 1)
-        quantise_x(0, 0, 0)
-        quantise_rest(2, 0, count=2)
-        half_products((0, 1, 2, 3), 0, 0, 0, both)
-        subtract(0, 1)
-        quantise_rest(4, 0)
-        half_products((4,), 0, 0, 0, both)
-        quantise_x(0, 1, 0)
-        subtract(1, 1)
-        quantise_w(4, 1)
-        half_products(left, 0, 1, 0, both)
-        expand(4, 1)
+        def QI(lo=0, hi=4):
+            def call():
+                nc.vector.quantize_mx(
+                    out=id_codes[:, lo * P : hi * P].bitcast(FP8X4), scales=id_scales[:, lo * P : hi * P],
+                    in_=identity[:, lo * K_PASS : hi * K_PASS],
+                )
+            return (call, [], [("identity", j) for j in range(lo, hi)])
 
-        round_x(scalar, 0, 0, 1, count=2)
-        round_x(scalar, 0, 2, 1, count=2)
-        subtract(2, 1)
-        quantise_rest(0, 1, count=2)
-        quantise_x(0, 0, 1)
-        subtract(3, 1)
-        quantise_rest(2, 1)
-        half_products(left, 0, 0, 1, (0,))
-        half_products((0, 1, 2), 0, 0, 1, (1,))
-        quantise_x(0, 1, 1)
-        subtract(4, 1)
-        quantise_rest(3, 1)
-        quantise_rest(4, 1)
-        half_products((0, 1, 2), 0, 1, 1, both)
-        half_products((3, 4), 0, 1, 1, (0,))
-        products((3, 4), (0,), 1, (1,))
 
-        round_x(scalar, 1, 0, 0, count=2)
-        round_x(scalar, 1, 2, 0, count=2)
-        quantise_x(1, 0, 0)
-        relu_chunk(vector, 0, 0)
-        relu_chunk(scalar, 1, 0)
-        half_products(left, 1, 0, 0, both)
-        quantise_x(1, 1, 0)
-        half_products(left, 1, 1, 0, both)
-        round_x(vector, 1, 0, 1, count=2)
-        round_x(scalar, 1, 3, 1)
-        round_x(vector, 1, 2, 1)
-        quantise_x(1, 0, 1)
-        quantise_x(1, 1, 1)
-        for i in (2, 3, 4):
-            relu_chunk(scalar, i, 0)
-        square(scalar, 0, 0, CHUNK)
-        products((0, 1), (1,), 1, both)
-        round_w(vector, 5, 0)
-        round_w(vector, 6, 0)
-        quantise_w(5, 0)
-        round_w(vector, 7, 0)
-        quantise_w(6, 0)
-        expand(5, 0)
-        products((2,), (1,), 1, both)
-        expand(6, 0)
-        round_w(vector, 5, 1)
-        quantise_w(7, 0)
-        round_w(vector, 6, 1)
-        quantise_w(5, 1)
-        products((3,), (1,), 1, both)
-        expand(5, 1)
-        subtract(5, 0)
-        quantise_w(6, 1)
-        products((4,), (1,), 1, both)
-        expand(6, 1)
-        relu_chunk(scalar, 0, 1)
-        relu_chunk(scalar, 1, 1)
-        square(scalar, 0, CHUNK, 2 * CHUNK)
-        store(0, 0, 2 * CHUNK)
-        relu_chunk(scalar, 2, 1)
+        def RV(n, g, lo, hi=None):
+            return rnd(V, n, g, lo, hi or lo + 1)
+        def RS(n, g, lo, hi=None):
+            return rnd(S, n, g, lo, hi or lo + 1)
+        def RG(n, g, lo, hi=None):
+            return rnd(G, n, g, lo, hi or lo + 1)
+        def Q(g, lo, hi=None):
+            return quant("w_q", g, lo, hi or lo + 1)
+        def QR(g, lo, hi=None):
+            return quant("w_r", g, lo, hi or lo + 1)
+        def QX(g, lo, hi=None):
+            return quant("x", g, lo, hi or lo + 2)
 
-        early = (0, 1)
-        subtract(6, 0)
-        quantise_rest(5, 0)
-        round_w(vector, 7, 1)
-        subtract(5, 1)
-        quantise_rest(6, 0)
-        quantise_w(7, 1)
-        for g in range(PASSES):
-            products((5,), early, g, (0,))
-        expand(7, 0)
-        relu_chunk(scalar, 3, 1)
-        square(scalar, 1, 0, 2 * CHUNK)
-        store(1, 0, 2 * CHUNK)
-        relu_chunk(scalar, 4, 1)
-        subtract(6, 1)
-        quantise_rest(5, 1)
-        products((5,), early, 0, (1,))
-        expand(7, 1)
-        products((5,), early, 1, (1,))
-        round_x(vector, 2, 0, 0, count=2)
-        quantise_rest(6, 1)
-        subtract(7, 0)
-        round_x(vector, 2, 2, 0, count=2)
-        quantise_rest(7, 0)
-        subtract(7, 1)
-        quantise_x(2, 0, 0)
-        quantise_rest(7, 1)
-        quantise_x(2, 1, 0)
-        for i in (6, 7):
-            for g in range(PASSES):
-                products((i,), early, g, both)
-        round_x(vector, 2, 0, 1, count=2)
-        round_x(vector, 2, 2, 1, count=2)
-        for i in (2, 3, 4):
-            square(scalar, i, 0, 2 * CHUNK)
-            store(i, 0, 2 * CHUNK)
-        quantise_x(2, 0, 1)
-        quantise_x(2, 1, 1)
-
-        for t in early:
-            relu_chunk(scalar, 5, t)
-        relu_chunk(scalar, 6, 0)
-        square(scalar, 5, 0, 2 * CHUNK)
-        store(5, 0, 2 * CHUNK)
-        relu_chunk(vector, 6, 1)
-        relu_chunk(vector, 7, 0)
-        square(vector, 6, 0, 2 * CHUNK)
-        store(6, 0, 2 * CHUNK)
-        relu_chunk(scalar, 7, 1)
-        square(scalar, 7, 0, CHUNK)
-        square(vector, 7, CHUNK, 2 * CHUNK)
-        store(7, 0, 2 * CHUNK)
-        last = 2 * CHUNK
-        for g in range(PASSES):
-            products((0, 1), (2,), g, both)
-        for i in (0, 1):
-            finish(i, last, T)
-        pieces = [(i, last, T) for i in (2, 3, 4)]
-        pieces.extend((i, lo, lo + HALF) for i in (5, 6) for lo in (last, last + HALF))
-        pieces.extend([(7, last, last + HALF), (7, last + HALF, T - P), (7, T - P, T)])
-        for i, lo, hi in pieces:
-            for g in range(PASSES):
-                for tier in both:
-                    product(i, g, tier, lo, hi, lo, hi - lo)
-            finish(i, lo, hi)
+        for panel in (("w",0,0,2),("w",0,2,4),("w",0,4,6),("x",0,0,2),("w",1,0,2),("x",0,2,4),("w",1,2,4),("x",1,0,2),("w",1,4,6),("x",1,2,4),("x",0,4,6),("x",0,6,8),("x",1,4,8),("w",0,6,8),("w",1,6,8),("x",0,8,12),("x",1,8,12),):
+            load(*panel)
+        make_identity()
+        for i, lo, hi, bank in ((0,0,4,0),(1,0,4,1),(2,0,4,2),(3,0,4,3),(4,0,4,4),(5,0,4,5),(0,4,8,6),(1,4,8,7),(2,4,8,0),(3,4,8,1),(4,4,8,2),(5,4,8,3),(6,0,4,6),(6,4,8,7),(7,0,4,0),(7,4,8,1),(0,8,12,4),(1,8,12,5),(2,8,12,2),(3,8,12,3),(4,8,10,6),(4,10,12,7),(5,8,10,0),(5,10,12,1),(6,8,10,4),(6,10,12,5),(7,8,9,2),(7,9,10,3),(7,10,11,6),(7,11,12,7),):
+            place(i, lo, hi, bank)
+        tq = [expand(0,0,6), expand(1,0,7), expand(2,0,2), expand(3,0,3), expand(4,0,4), expand(5,0,5), *mms((0,1,2,),0,both,0,2), expand(0,1,6), *mms((3,),0,both,0,2), *mms((4,5,),0,(0,),0,2), *mms((4,),0,(1,),0,2), expand(1,1,7), *mms((5,),0,(1,),0,2), *mms((0,1,2,),0,both,2,4), expand(2,1,6), *mms((3,4,),0,both,2,4), expand(3,1,7), *mms((5,),0,both,2,4), *mms((0,1,),1,both,0,1), *mms((2,3,),1,(0,),0,1), *mms((0,1,),1,both,1,2), *mms((2,3,),1,(0,),1,2), expand(4,1,6), *mms((2,),1,(1,),0,2), *mms((4,),1,(0,),0,2), expand(5,1,7), *mms((5,),1,(0,),0,2), *mms((3,),1,(1,),0,2), *mms((0,1,2,3,),1,both,2,3), *mms((0,1,2,3,),1,both,3,4), *mms((4,5,),1,(0,),2,4), *mms((4,),1,(1,),0,4), *mms((0,),0,both,4,6), *mms((5,),1,(1,),0,4), *mms((1,2,3,4,5,),0,both,4,6), *mms((0,1,2,3,4,5,),0,both,6,8), *mms((0,1,),1,both,4,8), expand(6,0,4), *mms((2,),1,both,4,8), expand(7,0,5), *mms((3,4,),1,both,4,8), expand(6,1,4), *mms((5,),1,both,4,8), expand(7,1,5), *mms((6,),0,both,0,4), *mms((6,),0,both,4,8), *mms((6,),1,(0,),0,4), *mms((6,),1,(0,),4,8), *mms((7,),0,both,0,4), *mms((6,),1,(1,),0,4), *mms((6,),1,(1,),4,8), *mms((7,),0,both,4,8), *mms((7,),1,both,0,4), *mms((7,),1,both,4,8), *mms((0,1,),0,both,8,12), *mms((0,1,),1,both,8,12), *mms((2,),0,both,8,12), *mms((2,),1,both,8,12), *mms((3,),0,both,8,12), *mms((3,),1,both,8,12), *mms((4,),0,both,8,10), *mms((4,),1,both,8,10), *mms((4,),0,both,10,12), *mms((4,),1,both,10,12), *mms((5,),0,both,8,10), *mms((5,),1,both,8,10), *mms((5,),0,both,10,12), *mms((5,),1,both,10,12), *mms((6,),0,both,8,10), *mms((6,),1,both,8,10), *mms((6,),0,both,10,12), *mms((6,),1,both,10,12), *mms((7,),0,both,8,9), *mms((7,),1,both,8,9), *mms((7,),0,both,9,10), *mms((7,),1,both,9,10), *mms((7,),0,both,10,11), *mms((7,),1,both,10,11), *mms((7,),0,both,11,12), *mms((7,),1,both,11,12)]
+        vq = [QI(0,2), RV("w",0,0), QI(2,4), Q(0,0), Q(0,1), RV("w",0,2), Q(0,2), sub(0,0), Q(0,3), sub(1,0), QR(0,0), Q(0,4), sub(2,0), QR(0,1), Q(0,5), sub(3,0), QR(0,2), QX(0,0), sub(4,0), QR(0,3), Q(1,0), sub(5,0), QR(0,4), Q(1,1), QR(0,5), QX(0,2), sub(0,1), Q(1,2), sub(1,1), QR(1,0), Q(1,3), QR(1,1), QX(1,0,1), sub(2,1), QX(1,1,2), Q(1,4), QR(1,2), sub(3,1), Q(1,5), QR(1,3), QX(1,2,3), sub(4,1), QX(1,3,4), sub(5,1), QR(1,4), QX(0,4), QR(1,5), relu(V,0,0), relu(V,1,0), QX(0,6), RV("x",1,4,6), QX(1,4), RV("w",0,6), QX(1,6), RV("w",0,7), Q(0,6), Q(0,7), RV("w",1,6), RV("w",1,7), Q(1,6), relu(V,0,4), sub(6,0), Q(1,7), sub(7,0), QR(0,6), RV("x",0,8,10), QR(0,7), sub(6,1), RV("x",0,10,12), QR(1,6), sub(7,1), QX(0,8), QR(1,7), QX(0,10), RV("x",1,8,10), RV("x",1,10,12), QX(1,8), QX(1,10), relu(V,6,0), relu(V,6,4), square(V,6,0,4), relu(V,7,4), square(V,7,0,4), square(V,7,4,8), square(V,0,8,12), square(V,1,8,12), square(V,2,8,12), square(V,3,8,12), square(V,4,8,10), square(V,4,10,12), square(V,5,8,10), square(V,5,10,12), square(V,6,8,10), square(V,6,10,12), square(V,7,8,9), square(V,7,9,10), square(V,7,10,11), square(V,7,11,12)]
+        sq = [RS("w",0,1), RS("w",0,3), RS("w",0,4), RS("w",0,5), RS("x",0,0,2), RS("w",1,0), RS("w",1,1), RS("x",0,2,4), RS("w",1,2), RS("w",1,3), RS("x",1,0), RS("x",1,1), RS("w",1,4), RS("w",1,5), RS("x",1,2), RS("x",1,3), RS("x",0,4,6), RS("x",0,6,8), relu(S,2,0), relu(S,3,0), RS("x",1,6,8), relu(S,4,0), relu(S,5,0), square(S,0,0,4), square(S,1,0,4), square(S,2,0,4), relu(S,1,4), square(S,0,4,8), relu(S,2,4), square(S,1,4,8), relu(S,3,4), square(S,2,4,8), square(S,3,0,4), relu(S,4,4), square(S,3,4,8), square(S,4,0,4), relu(S,5,4), square(S,4,4,8), square(S,5,0,8), relu(S,7,0), square(S,6,4,8), relu(S,0,8), relu(S,1,8), relu(S,2,8), relu(S,3,8), relu(S,4,8), relu(S,4,10), relu(S,5,8), relu(S,5,10), relu(S,6,8), relu(S,6,10), relu(S,7,8), relu(S,7,9), relu(S,7,10), relu(S,7,11)]
+        gq = []
+        dq = [store(0,0,8), store(1,0,8), store(2,0,8), store(3,0,8), store(4,0,8), store(5,0,8), store(6,0,8), store(7,0,8), store(0,8,12), store(1,8,12), store(2,8,12), store(3,8,12), store(4,8,10), store(4,10,12), store(5,8,10), store(5,10,12), store(6,8,10), store(6,10,12), store(7,8,9), store(7,9,10), store(7,10,11), store(7,11,12)]
+        issue([tq, vq, sq, gq, dq])

from contextlib import ExitStack

import concourse.mybir as mybir

K, N, T = 1024, 1024, 1536
FLOPS = 2 * 2 * K * N * T

F32 = mybir.dt.float32
BF16 = mybir.dt.bfloat16
U32 = mybir.dt.uint32
U8 = mybir.dt.uint8
FP8X4 = mybir.dt.float8_e4m3fn_x4
ALU = mybir.AluOpType
ACT = mybir.ActivationFunctionType

P = 128
PACK = 4
K_PASS = P * PACK
PASSES = K // K_PASS
TIERS = 2
BANDS = N // P
CHUNK = 4
RUN = 4
SCALAR_PART = 3


def tile_mix_tierw_relu2_kernel(tc, w, x, out):
    nc = tc.nc
    with ExitStack() as ctx:
        keep = ctx.enter_context(tc.tile_pool(name="keep", bufs=1))
        psum = ctx.enter_context(tc.psum_pool(name="psum", bufs=1))
        ctx.enter_context(tc.manual_schedule())

        raw, expanded, sums, columns_left, result = {}, {}, {}, {}, {}
        grouped, codes, scales = {}, {}, {}
        for g in range(PASSES):
            for name, width in (("w", N), ("x", T)):
                grouped[name, g] = keep.tile([P, PACK * width], BF16, name="grouped_%s%d" % (name, g), align_bytes=256)
            for name, width in (("w_q", N), ("w_r", N), ("x", T)):
                codes[name, g] = keep.tile([P, width], U32, name="codes_%s%d" % (name, g), align_bytes=256)
                scales[name, g] = keep.tile([P, width], U8, name="scales_%s%d" % (name, g), align_bytes=256)
        for i in range(BANDS):
            result[i] = keep.tile([P, T], F32, name="res_%d" % i, align_bytes=256)
        identity = keep.tile([P, PACK * K_PASS], BF16, name="ident", align_bytes=256)
        id_codes = keep.tile([P, K_PASS], U32, name="id_codes", align_bytes=256)
        id_scales = keep.tile([P, K_PASS], U8, name="id_scales", align_bytes=256)

        def rows_view(ap):
            return ap.rearrange("p j (c i) -> p c j i", i=RUN)

        def words_view(ap):
            return ap.rearrange("p (c i j) -> p c j i", i=RUN, j=PACK)

        def load(name, g, lo, hi):
            src = w if name == "w" else x
            tile = keep.tile([P, PACK, (hi - lo) * P], F32, name="raw_%s_%d_%d" % (name, lo, g), align_bytes=256)
            rows = src[g * K_PASS : (g + 1) * K_PASS, lo * P : hi * P]
            nc.sync.dma_start(out=tile[:], in_=rows.rearrange("(p j) n -> p j n", j=PACK))
            for s in range(lo, hi):
                raw[name, g, s] = (tile, lo)

        def raw_columns(name, g, lo, hi):
            tile, first = raw[name, g, lo]
            return tile[:, :, (lo - first) * P : (hi - first) * P]

        def rnd(engine, name, g, lo, hi):
            def call():
                dst = words_view(grouped[name, g][:, K_PASS * lo : K_PASS * hi])
                src = rows_view(raw_columns(name, g, lo, hi))
                if engine is nc.vector:
                    nc.vector.tensor_copy(out=dst, in_=src)
                elif engine is nc.scalar:
                    nc.scalar.copy(out=dst, in_=src)
                else:
                    nc.gpsimd.tensor_scalar(out=dst, in0=src, scalar1=1.0, scalar2=0.0, op0=ALU.mult, op1=ALU.add)
            return (call, [], [("rounded", name, g, s) for s in range(lo, hi)])

        def quant(name, g, lo, hi):
            def call():
                nc.vector.quantize_mx(
                    out=codes[name, g][:, lo * P : hi * P].bitcast(FP8X4),
                    scales=scales[name, g][:, lo * P : hi * P],
                    in_=grouped[name[0], g][:, K_PASS * lo : K_PASS * hi],
                )
            source = {"w_q": "w", "w_r": "rest", "x": "x"}[name]
            return (call, [("rounded", source, g, s) for s in range(lo, hi)], [(name, g, s) for s in range(lo, hi)])

        busy = set()

        def expand(i, g, bank):
            def call():
                expanded[i, g] = (psum.tile([P, PACK, P], F32, name="bank_%d" % bank), bank)
                busy.add(bank)
                for j in range(PACK):
                    nc.tensor.matmul_mx(
                        out=expanded[i, g][0][:, j, :],
                        lhsT=id_codes[:, j * P : (j + 1) * P].bitcast(FP8X4),
                        lhsT_scale=id_scales[:, j * P : (j + 1) * P],
                        rhs=codes["w_q", g][:, i * P : (i + 1) * P].bitcast(FP8X4),
                        rhs_scale=scales["w_q", g][:, i * P : (i + 1) * P],
                        start=True,
                        stop=True,
                    )
            return (call, [("w_q", g, i), ("bank", bank)] + [("identity", j) for j in range(PACK)], [("expanded", g, i)])

        def sub(i, g):
            def call():
                tile, bank = expanded[i, g]
                nc.vector.tensor_tensor(
                    out=words_view(grouped["w", g][:, K_PASS * i : K_PASS * (i + 1)]),
                    in0=rows_view(raw_columns("w", g, i, i + 1)),
                    in1=rows_view(tile[:]),
                    op=ALU.subtract,
                )
                busy.remove(bank)
            return (call, [("expanded", g, i)], [("rounded", "rest", g, i)])

        home = {}

        def place(i, lo, hi, bank):
            for s in range(lo, hi):
                home[i, s] = (lo, hi, bank)

        opened = set()

        def mm(i, g, tier, lo, hi):
            first, end, bank = home[i, lo]
            key = (i, first)
            start = key not in opened
            opened.add(key)
            columns_left[key] = columns_left.get(key, TIERS * PASSES * (end - first)) - (hi - lo)
            stop = columns_left[key] == 0
            operand = (("w_q", "w_r")[tier], g)

            def call():
                if start:
                    sums[key] = psum.tile([P, (end - first) * P], F32, name="bank_%d" % bank)
                    busy.add(bank)
                nc.tensor.matmul_mx(
                    out=sums[key][:, (lo - first) * P : (hi - first) * P],
                    lhsT=codes[operand][:, i * P : (i + 1) * P].bitcast(FP8X4),
                    lhsT_scale=scales[operand][:, i * P : (i + 1) * P],
                    rhs=codes["x", g][:, lo * P : hi * P].bitcast(FP8X4),
                    rhs_scale=scales["x", g][:, lo * P : hi * P],
                    start=start,
                    stop=stop,
                )
            needs = [operand + (i,)] + [("x", g, s) for s in range(lo, hi)] + ([("bank", bank)] if start else [])
            return (call, needs, [("summed", i, first)] if stop else [])

        def relu(engine, i, lo):
            first, end, bank = home[i, lo]

            def call():
                dst = result[i][:, first * P : end * P]
                if engine is nc.vector:
                    nc.vector.tensor_scalar_max(out=dst, in0=sums[i, first][:], scalar1=0.0)
                else:
                    nc.scalar.activation(out=dst, in_=sums[i, first][:], func=ACT.Relu)
                busy.remove(bank)
            return (call, [("summed", i, first)], [("positive", i, s) for s in range(first, end)])

        def square(engine, i, lo, hi):
            def call():
                dst = result[i][:, lo * P : hi * P]
                if engine is nc.scalar:
                    nc.scalar.activation(out=dst, in_=dst, func=ACT.Square)
                else:
                    engine.tensor_tensor(out=dst, in0=dst, in1=dst, op=ALU.mult)
            return (call, [("positive", i, s) for s in range(lo, hi)], [("squared", i, s) for s in range(lo, hi)])

        def store(i, lo, hi):
            def call():
                nc.sync.dma_start(out=out[i * P : (i + 1) * P, lo * P : hi * P], in_=result[i][:, lo * P : hi * P])
            return (call, [("squared", i, s) for s in range(lo, hi)], [])

        def issue(queues):
            facts = set()
            at = [0] * len(queues)
            while any(at[q] < len(queues[q]) for q in range(len(queues))):
                moved = False
                for q in range(len(queues)):
                    while at[q] < len(queues[q]):
                        call, needs, makes = queues[q][at[q]]
                        if not all((f[1] not in busy) if f[0] == "bank" else (f in facts) for f in needs):
                            break
                        call()
                        for f in makes:
                            facts.add(f)
                        at[q] = at[q] + 1
                        moved = True
                assert moved, at

        V, S, G = nc.vector, nc.scalar, nc.gpsimd
        both = (0, 1)

        def mms(bands, g, tiers, lo, hi):
            return [mm(i, g, tier, lo, hi) for i in bands for tier in tiers]

        def make_identity():
            one_hot = keep.tile([P, K_PASS + PACK], BF16, name="ramp")
            nc.gpsimd.memset(one_hot[:].bitcast(U32), 0)
            nc.gpsimd.affine_select(
                out=one_hot[:], in_=one_hot[:], compare_op=ALU.not_equal, fill=1.0,
                base=PACK - 1, pattern=[[-1, K_PASS + PACK]], channel_multiplier=PACK,
            )
            for j in range(PACK):
                dst = identity[:, j * K_PASS : (j + 1) * K_PASS]
                src = one_hot[:, PACK - 1 - j : PACK - 1 - j + K_PASS]
                if j == SCALAR_PART:
                    nc.scalar.activation(out=dst, in_=src, func=ACT.Square)
                else:
                    nc.vector.tensor_copy(out=dst, in_=src)

        def QI(lo=0, hi=4):
            def call():
                nc.vector.quantize_mx(
                    out=id_codes[:, lo * P : hi * P].bitcast(FP8X4), scales=id_scales[:, lo * P : hi * P],
                    in_=identity[:, lo * K_PASS : hi * K_PASS],
                )
            return (call, [], [("identity", j) for j in range(lo, hi)])


        def RV(n, g, lo, hi=None):
            return rnd(V, n, g, lo, hi or lo + 1)
        def RS(n, g, lo, hi=None):
            return rnd(S, n, g, lo, hi or lo + 1)
        def RG(n, g, lo, hi=None):
            return rnd(G, n, g, lo, hi or lo + 1)
        def Q(g, lo, hi=None):
            return quant("w_q", g, lo, hi or lo + 1)
        def QR(g, lo, hi=None):
            return quant("w_r", g, lo, hi or lo + 1)
        def QX(g, lo, hi=None):
            return quant("x", g, lo, hi or lo + 2)

        for panel in (("w",0,0,2),("w",0,2,4),("w",0,4,6),("x",0,0,2),("w",1,0,2),("x",0,2,4),("w",1,2,4),("x",1,0,2),("w",1,4,6),("x",1,2,4),("x",0,4,6),("x",0,6,8),("x",1,4,8),("w",0,6,8),("w",1,6,8),("x",0,8,12),("x",1,8,12),):
            load(*panel)
        make_identity()
        for i, lo, hi, bank in ((0,0,4,0),(1,0,4,1),(2,0,4,2),(3,0,4,3),(4,0,4,4),(5,0,4,5),(0,4,8,6),(1,4,8,7),(2,4,8,0),(3,4,8,1),(4,4,8,2),(5,4,8,3),(6,0,4,6),(6,4,8,7),(7,0,4,0),(7,4,8,1),(0,8,12,4),(1,8,12,5),(2,8,12,2),(3,8,12,3),(4,8,10,6),(4,10,12,7),(5,8,10,0),(5,10,12,1),(6,8,10,4),(6,10,12,5),(7,8,9,2),(7,9,10,3),(7,10,11,6),(7,11,12,7),):
            place(i, lo, hi, bank)
        tq = [expand(0,0,6), expand(1,0,7), expand(2,0,2), expand(3,0,3), expand(4,0,4), expand(5,0,5), *mms((0,1,2,),0,both,0,2), expand(0,1,6), *mms((3,),0,both,0,2), *mms((4,5,),0,(0,),0,2), *mms((4,),0,(1,),0,2), expand(1,1,7), *mms((5,),0,(1,),0,2), *mms((0,1,2,),0,both,2,4), expand(2,1,6), *mms((3,4,),0,both,2,4), expand(3,1,7), *mms((5,),0,both,2,4), *mms((0,1,),1,both,0,1), *mms((2,3,),1,(0,),0,1), *mms((0,1,),1,both,1,2), *mms((2,3,),1,(0,),1,2), expand(4,1,6), *mms((2,),1,(1,),0,2), *mms((4,),1,(0,),0,2), expand(5,1,7), *mms((5,),1,(0,),0,2), *mms((3,),1,(1,),0,2), *mms((0,1,2,3,),1,both,2,3), *mms((0,1,2,3,),1,both,3,4), *mms((4,5,),1,(0,),2,4), *mms((4,),1,(1,),0,4), *mms((0,),0,both,4,6), *mms((5,),1,(1,),0,4), *mms((1,2,3,4,5,),0,both,4,6), *mms((0,1,2,3,4,5,),0,both,6,8), *mms((0,1,),1,both,4,8), expand(6,0,4), *mms((2,),1,both,4,8), expand(7,0,5), *mms((3,4,),1,both,4,8), expand(6,1,4), *mms((5,),1,both,4,8), expand(7,1,5), *mms((6,),0,both,0,4), *mms((6,),0,both,4,8), *mms((6,),1,(0,),0,4), *mms((6,),1,(0,),4,8), *mms((7,),0,both,0,4), *mms((6,),1,(1,),0,4), *mms((6,),1,(1,),4,8), *mms((7,),0,both,4,8), *mms((7,),1,both,0,4), *mms((7,),1,both,4,8), *mms((0,1,),0,both,8,12), *mms((0,1,),1,both,8,12), *mms((2,),0,both,8,12), *mms((2,),1,both,8,12), *mms((3,),0,both,8,12), *mms((3,),1,both,8,12), *mms((4,),0,both,8,10), *mms((4,),1,both,8,10), *mms((4,),0,both,10,12), *mms((4,),1,both,10,12), *mms((5,),0,both,8,10), *mms((5,),1,both,8,10), *mms((5,),0,both,10,12), *mms((5,),1,both,10,12), *mms((6,),0,both,8,10), *mms((6,),1,both,8,10), *mms((6,),0,both,10,12), *mms((6,),1,both,10,12), *mms((7,),0,both,8,9), *mms((7,),1,both,8,9), *mms((7,),0,both,9,10), *mms((7,),1,both,9,10), *mms((7,),0,both,10,11), *mms((7,),1,both,10,11), *mms((7,),0,both,11,12), *mms((7,),1,both,11,12)]
        vq = [QI(0,2), RV("w",0,0), QI(2,4), Q(0,0), Q(0,1), RV("w",0,2), Q(0,2), sub(0,0), Q(0,3), sub(1,0), QR(0,0), Q(0,4), sub(2,0), QR(0,1), Q(0,5), sub(3,0), QR(0,2), QX(0,0), sub(4,0), QR(0,3), Q(1,0), sub(5,0), QR(0,4), Q(1,1), QR(0,5), QX(0,2), sub(0,1), Q(1,2), sub(1,1), QR(1,0), Q(1,3), QR(1,1), QX(1,0,1), sub(2,1), QX(1,1,2), Q(1,4), QR(1,2), sub(3,1), Q(1,5), QR(1,3), QX(1,2,3), sub(4,1), QX(1,3,4), sub(5,1), QR(1,4), QX(0,4), QR(1,5), relu(V,0,0), relu(V,1,0), QX(0,6), RV("x",1,4,6), QX(1,4), RV("w",0,6), QX(1,6), RV("w",0,7), Q(0,6), Q(0,7), RV("w",1,6), RV("w",1,7), Q(1,6), relu(V,0,4), sub(6,0), Q(1,7), sub(7,0), QR(0,6), RV("x",0,8,10), QR(0,7), sub(6,1), RV("x",0,10,12), QR(1,6), sub(7,1), QX(0,8), QR(1,7), QX(0,10), RV("x",1,8,10), RV("x",1,10,12), QX(1,8), QX(1,10), relu(V,6,0), relu(V,6,4), square(V,6,0,4), relu(V,7,4), square(V,7,0,4), square(V,7,4,8), square(V,0,8,12), square(V,1,8,12), square(V,2,8,12), square(V,3,8,12), square(V,4,8,10), square(V,4,10,12), square(V,5,8,10), square(V,5,10,12), square(V,6,8,10), square(V,6,10,12), square(V,7,8,9), square(V,7,9,10), square(V,7,10,11), square(V,7,11,12)]
        sq = [RS("w",0,1), RS("w",0,3), RS("w",0,4), RS("w",0,5), RS("x",0,0,2), RS("w",1,0), RS("w",1,1), RS("x",0,2,4), RS("w",1,2), RS("w",1,3), RS("x",1,0), RS("x",1,1), RS("w",1,4), RS("w",1,5), RS("x",1,2), RS("x",1,3), RS("x",0,4,6), RS("x",0,6,8), relu(S,2,0), relu(S,3,0), RS("x",1,6,8), relu(S,4,0), relu(S,5,0), square(S,0,0,4), square(S,1,0,4), square(S,2,0,4), relu(S,1,4), square(S,0,4,8), relu(S,2,4), square(S,1,4,8), relu(S,3,4), square(S,2,4,8), square(S,3,0,4), relu(S,4,4), square(S,3,4,8), square(S,4,0,4), relu(S,5,4), square(S,4,4,8), square(S,5,0,8), relu(S,7,0), square(S,6,4,8), relu(S,0,8), relu(S,1,8), relu(S,2,8), relu(S,3,8), relu(S,4,8), relu(S,4,10), relu(S,5,8), relu(S,5,10), relu(S,6,8), relu(S,6,10), relu(S,7,8), relu(S,7,9), relu(S,7,10), relu(S,7,11)]
        gq = []
        dq = [store(0,0,8), store(1,0,8), store(2,0,8), store(3,0,8), store(4,0,8), store(5,0,8), store(6,0,8), store(7,0,8), store(0,8,12), store(1,8,12), store(2,8,12), store(3,8,12), store(4,8,10), store(4,10,12), store(5,8,10), store(5,10,12), store(6,8,10), store(6,10,12), store(7,8,9), store(7,9,10), store(7,10,11), store(7,11,12)]
        issue([tq, vq, sq, gq, dq])
